import numpy as np, ml_dtypes
CORES = [9,25,41,57]
N = 4
BF = ml_dtypes.bfloat16
W, TU, RO, Q, S = 8192, 256, 5, 9, 32
HOPS = [1]
BL = TU // len(HOPS)
def pack(x, l, w, k, h):
    return {"field": x.reshape(N, 128, W).astype(np.float32).astype(BF), "tube": np.ascontiguousarray(l.reshape(N, 128, TU)).astype(np.int32),
            "wt": w.reshape(N, 128, 1).astype(np.int32), "kn": k.reshape(N, 128, 1).astype(np.int32), "lim": np.ascontiguousarray(h.reshape(N, 128, RO)).astype(np.int32)}
def parts(rng):
    dark = rng.random((N, 8, 1, W)) < rng.choice(np.array([0.04, 0.08, 0.15]), (N, 8, 1, 1))
    x = np.where(dark, rng.integers(0, 64, (N, 8, 16, W), dtype=np.int16), rng.integers(48, 256, (N, 8, 16, W), dtype=np.int16))
    l = rng.integers(0, W, (N, 8, 16, TU)); w = rng.integers(0, 256, (N, 8, 16)); k = rng.integers(0, 256, (N, 8, 16))
    return x, l, w, k, rng.integers(16, 72, (N, 8, 16, RO))
def setup_inputs(rng):
    return pack(*parts(rng))
def setup_inputs_spread(rng):
    sh = rng.choice(np.array([0, 0, 0, 0, 0, 1, 1, 2, 4, 8], np.int16), (N, 8, 1, W))
    x = rng.integers(0, 256, (N, 8, 16, W), dtype=np.int16) >> sh
    l = rng.integers(0, W, (N, 8, 16, TU)); l[:, 1::2] = np.minimum((W * rng.random((N, 4, 16, TU)) ** 3).astype(np.int64), W - 1)
    w = rng.integers(0, 256, (N, 8, 16)) >> rng.integers(0, 9, (N, 8, 16)); k = rng.integers(0, 256, (N, 8, 16)) >> rng.integers(0, 9, (N, 8, 16))
    h = rng.integers(0, 249, (N, 8, 16, RO)) >> rng.integers(0, 9, (N, 8, 1, RO))
    return pack(x, l, w, k, h)
def ends_of(rng, hi, shape):
    return np.where(rng.random(shape) < 0.14, rng.integers(0, hi + 1, shape), hi * rng.integers(0, 2, shape))
def setup_inputs_ends(rng):
    kind = rng.random((N, 8, 1, W)); top = np.int16(255)
    x = np.where(kind < 0.7, top, np.where(kind < 0.82, np.int16(0), top * rng.integers(0, 2, (N, 8, 16, W), dtype=np.int16)))
    i = np.arange(16)[:, None]
    b = ((np.arange(N)[:, None] + np.arange(8)[None, :]) & 1) * (W - 1)
    l = np.where(i < rng.integers(0, 17, (N, 8, 1, TU)), b[:, :, None, None], (W - 1) * rng.integers(0, 2, (N, 8, 16, TU)))
    free = ((np.arange(TU) * 5) & 15) < 5; l[..., free] = rng.integers(0, W, (N, 8, 16, int(np.count_nonzero(free))))
    w = ends_of(rng, 255, (N, 8, 16)); k = ends_of(rng, 255, (N, 8, 16))
    h = 248 * rng.integers(0, 2, (N, 8, 16, RO)); h[:, 1::2] = 248 * rng.integers(0, 2, (N, 4, 1, RO))
    for q in range(N):
        for g in range(8):
            o = W - 1 - b[q, g]; x[q, g][:, b[q, g]] = 255
            x[q, g][:, o] = 0 if (g & 3) < 2 or q == 1 else 255 * rng.integers(0, 2, 16) if (g & 3) == 2 else 255
    h[0, :, :, 0] = 0; h[0, 0, :, 1] = 248; h[1, :, :, 0] = 248; h[1, 0, :, 1] = 0; l[1, :, 15, :] = (W - 1 - b[1])[:, None]
    h[2, :, :, 0] = 0; h[2, 0, :, 0] = 248; l[2, 0] = b[2, 0]; l[2, 0, 15, :7] = W - 1 - b[2, 0]; h[2, :, :, 1] = 248
    p = N - 1; u = (15 * 65025) & 4095
    for g in range(4, 8):
        x[p, g][:, 0] = 255; x[p, g][:, W - 1] = 255; w[p, g] = 255
        if g == 5: w[p, g] = 0; w[p, g, 0] = 16; w[p, g, 1] = 1; x[p, g, 1, 0] = 15; x[p, g, 1, W - 1] = 15
        if g > 5:
            w[p, g, 0] = 0; k[p, g] = 255 * (np.arange(16) & 1)
            for j in (0, W - 1):
                x[p, g][:, ((u * u >> 4) + j) & (W - 1)] = 0
                x[p, g][:, ((u * u >> 4) + 255 * u + j) & (W - 1)] = 255 if g == 6 else 0
    return pack(x, l, w, k, h)
def setup_inputs_corners(rng):
    x, l, w, k, h = parts(rng); i = np.arange(16)[:, None]; v = np.arange(TU)
    for q in range(N):
        for g in range(8):
            c = (g + q) & 7
            if c == 0: h[q, g] = 0
            if c == 1: h[q, g] = 248; x[q, g] = np.minimum(x[q, g], 247)
            if c == 2:
                s = rng.integers(0, W, TU); s[0] = 0; s[1] = W - 1; l[q, g] = s[None, :]
            if c == 3:
                m = np.where(rng.random(W) < 0.9, Q, Q - 1)[None, :]
                x[q, g] = np.where(i < m, rng.integers(150, 256, (16, W)), rng.integers(0, 90, (16, W))); h[q, g] = 100
            if c == 4: w[q, g] = 0; k[q, g] = 0
            if c == 5:
                m = rng.random(W) < 0.9; x[q, g, 0, m] = 255; x[q, g, 1, m] = 15; w[q, g] = 0; w[q, g, 0] = 16; w[q, g, 1] = 1; k[q, g] = 255 * rng.integers(0, 2, 16)
            if c == 6:
                t = rng.integers(0, 4, (16, TU)); l[q, g] = np.where(t == 0, 0, np.where(t == 1, W - 1, np.where(t == 2, S * v, S * v + S - 1)))
            if c == 7:
                x[q, g][:, 0::2] = rng.integers(200, 256, (16, W // 2)); x[q, g][:, 1::2] = rng.integers(0, 64, (16, W // 2)); h[q, g] = 100
                l[q, g] = 2 * rng.integers(0, W // 2, (16, TU)) + (i == (v % 17)[None, :])
    return pack(x, l, w, k, h)
def setup_inputs_ties(rng):
    x, l, w, k, h = parts(rng)
    pr = 60 + 4 * rng.integers(0, 3, (N, 8, 16, 5)); x = np.take_along_axis(pr, np.broadcast_to(rng.integers(0, 5, (N, 8, 1, W)), (N, 8, 16, W)), 3)
    return pack(x, l, w, k, rng.integers(53, 66, (N, 8, 16, RO)))
def setup_inputs_brink(rng):
    x, l, w, k, h = parts(rng); r0 = int(rng.integers(0, 8)); v = np.arange(TU)
    h[..., 0] = 0; h[..., 1] = 248; h[..., 2:] = rng.integers(246, 249, (N, 8, 1, RO - 2))
    for g in range(8):
        c = (g + r0) & 7; low = rng.permutation(W)[:32]
        for q in range(N):
            if c < 4:
                o = rng.permutation(16); y = np.full((16, W), 254); y[o[:Q]] = 255
                b = np.nonzero(rng.random(W) < 0.1)[0]; y[o[rng.integers(0, Q, len(b))], b] = 254
                x[q, g] = y
            elif c < 6:
                x[q, g] = rng.integers(248, 256, (16, W)); x[q, g][:, low] = rng.integers(7, 9, (16, 32))
            else:
                x[q, g] = rng.integers(243, 256, (16, W)); x[q, g][:, low] = rng.integers(0, 4, (16, 32))
            if c >= 4:
                l[q, g, rng.integers(1, 16, TU), v] = low[rng.integers(0, 32, TU)]; h[q, g] = 0
            if c == 0:
                d = int(rng.integers(0, W)); s = rng.integers(0, W - 1, (16, TU)); l[q, g] = s + (s >= d)
                l[q, g, rng.integers(1, 16, 7), rng.permutation(TU)[:7]] = d
                x[q, g][:, d] = rng.integers(0, 248, 16); h[q, g, :, 0] = 248
    return pack(x, l, w, k, h)
def check_inputs(d):
    bad = []
    for a, lo, hi in (("field", 0, 255), ("tube", 0, W - 1), ("wt", 0, 255), ("kn", 0, 255), ("lim", 0, 248)):
        v = np.asarray(d[a]).astype(np.float64)
        if not (np.min(v) >= lo and np.max(v) <= hi): bad.append("range of " + a)
        elif np.any(v != np.floor(v)): bad.append("whole numbers of " + a)
    return bad
def reference(field, tube, wt, kn, lim):
    x = field.astype(np.float32).astype(np.int32).reshape(N, 8, 16, W)
    l = tube.astype(np.int64).reshape(N, 8, 16, TU)
    w = wt.astype(np.int64).reshape(N, 8, 16, 1); k = kn.astype(np.int64).reshape(N, 8, 16, 1); h = lim.astype(np.int64).reshape(N, 8, 16, RO)
    cut = [0] * N; v = np.arange(TU); j = np.arange(16)[:, None]
    for rnd in range(RO):
        if rnd: l = np.concatenate([np.roll(l[..., b * BL:(b + 1) * BL], HOPS[b], axis=0) for b in range(len(HOPS))], axis=-1)
        nl = np.zeros((N, 8, 16, TU), np.int64); nz = np.zeros((N, 8, 16, TU), np.int64); ncut = [0] * N
        for q in range(N):
            for g in range(8):
                X, L = x[q, g], l[q, g]
                M = np.minimum.accumulate(X[:, L], axis=1)
                holds = (M >= (h[q, g, :, rnd] + (cut[q] & 7))[:, None, None]).astype(np.int64)
                ok = (np.add.reduce(holds, axis=0) >= Q).astype(np.int64)
                m = np.maximum(np.add.reduce(ok, axis=0), 1) - 1
                Z = np.take_along_axis(M, np.broadcast_to(m[None, None, :], (16, 1, TU)), 1)[:, 0].astype(np.int64)
                u = np.add.reduce(w[q, g] * X[:, L[m, v]], axis=0) & 4095
                c = ((u * u >> 4)[None, :] + k[q, g] * u[None, :] + L) & (W - 1)
                s = np.add.reduce(np.abs(X[:, c] - Z[:, None, :]), axis=0)
                best = c[np.argmin(s, axis=0), v]
                back = L[np.clip(m[None, :] + 1 - j, 0, 15), v[None, :]]
                nl[q, g] = np.where(j == 0, best[None, :], np.where(j <= m[None, :], back, c)); nz[q, g] = Z
                y = (Z + X[:, best]) >> 1
                x[q, g][:, S * v + (u & (S - 1))] = y
                ncut[q] += int(np.count_nonzero(m < 15))
        l = nl; cut = ncut
    return {"yl": l.reshape(N, 128, TU).astype(np.float32), "yz": nz.reshape(N, 128, TU).astype(np.float32)}

@@ -1,0 +1,511 @@
+from concourse.mybir import AluOpType, AxisListType, ActivationFunctionType
+
+RO = 5
+CHUNKS = [(0, 128, [(0, 32), (32, 32), (64, 32), (96, 32)]), (128, 128, [(0, 32), (32, 32), (64, 32), (96, 32)])]
+UNIT = 64
+
+BF, F32, I32, U16 = "bfloat16", "float32", "int32", "uint16"
+SCRATCH = {"DL": ("dram", [8, 16, 256], F32), "irow": ("sbuf", [1, 128], BF), "c64": ("sbuf", [64, 128], BF)}
+for _n, _w, _d in (
+        ("X", 8192, BF), ("TI", 256, I32), ("wi", 1, I32), ("ki", 1, I32), ("li", 8, I32),
+        ("wc", 1, F32), ("kc", 1, F32), ("nl", 8, F32), ("lf", 8, F32), ("k2", 1, F32), ("k3", 1, F32), ("k4", 1, F32), ("sqb", 1, F32),
+        ("pI", 1, I32), ("iI", 1, I32), ("icol", 1, F32), ("i16", 1, F32), ("i32c", 1, F32),
+        ("pthr", 1, F32), ("pthv", 1, F32), ("ige1", 1, F32), ("e15", 1, F32),
+        ("ones", 128, BF), ("BO1", 128, BF), ("BO", 128, BF), ("IB", 128, BF), ("IF", 128, F32),
+        ("nI", 128, BF), ("n256I", 128, BF), ("pIm", 128, BF), ("nIm", 128, BF), ("WB", 128, BF), ("WB256", 128, BF),
+        ("S15", 128, BF), ("Sel0", 128, F32), ("LQ", 256, F32),
+        ("sel", 2048, BF), ("isel", 2048, BF), ("wsel", 2048, BF), ("sel256", 2048, BF), ("blk32", 8, BF), ("blkn", 8, BF),
+        ("v1i", 8, I32), ("v2i", 16, I32), ("v3i", 16, I32), ("VB", 8, BF), ("VW", 16, BF), ("SOp", 16, I32),
+        ("R01", 1024, BF), ("RB", 1024, BF), ("RK", 128, BF), ("half", 128, BF), ("W", 4096, F32),
+        ("soA", 16, I32), ("soB", 16, I32), ("soC", 16, I32), ("SO", 16, U16),
+        ("er", 1, F32), ("eI", 1, I32), ("eJ", 1, I32), ("nth", 8, F32), ("thv", 8, F32),
+        ("ZS", 4096, BF), ("G", 4096, BF), ("M", 4096, BF), ("H", 4096, BF), ("Zx", 4096, BF), ("D", 4096, BF), ("A", 4096, BF),
+        ("pas", 256, BF), ("OM", 16, U16), ("OW", 16, U16), ("OT", 16, U16), ("XL", 256, BF), ("Z2", 256, F32), ("B4", 256, BF),
+        ("SQ", 256, F32), ("xI", 256, I32), ("cI", 256, I32), ("CU", 256, U16), ("L32", 256, F32), ("OHA", 256, BF), ("sv", 256, BF),
+        ("OC", 256, F32), ("C1", 256, F32), ("R1", 256, F32), ("tt", 256, F32), ("Y2", 256, BF), ("yls", 256, F32), ("yzs", 256, F32)):
+    SCRATCH[_n] = ("sbuf", [128, _w], _d)
+for _c in range(2):
+    for _b in ("KM", "KS", "KB"):
+        SCRATCH["%s%d" % (_b, _c)] = ("sbuf", [128, 128], F32)
+    SCRATCH["OH%d" % _c] = ("sbuf", [128, 128], BF)
+    for _b in ("pb%d0", "pb%d1", "pb%d2", "pk%d"):
+        SCRATCH[_b % _c] = ("psum", [128, 512], F32)
+for _t in range(RO):
+    SCRATCH["LU%d" % _t] = ("sbuf", [128, 256], U16)
+    if _t < RO - 1:
+        SCRATCH["NU%d" % _t] = ("sbuf", [128, 256], U16)
+
+SEMAPHORES = ["cv", "cs", "ct", "cg", "sent", "ldt", "ldw", "ldk", "ldl", "ldx", "ldy", "dl", "w"] + \
+    ["%s%d" % (a, c) for a in ("oz", "ol") for c in range(len(CHUNKS))] + ["arr%d%d" % (t, c) for t in range(1, RO) for c in range(len(CHUNKS))]
+
+P = {"cyc": 0.83e-3 * 1.2, "ga": 1.6, "pec": 0.417e-3 * 1.2, "wake": 0.06, "hop": 3.5, "wdma": 6.0}
+PLACE = {}
+PRI = {}
+SIDES = "ssvsvvssssvsssssvsssvssssvvssssvvvssvsssvs"
+RANKS = """-348 -185 -40 78 -145 -186 -27 51 -54 -95 -114 108 93 -40 -323 100 -160 -231 -37 -244 -97 147 -103 123 -188 121 77 -166 -10 -17 70 13 85 -23 -38 -23 199 35 -22 244 35 -10 169 -114 -234 25 -153 -163 -7 -79 -139 17 47 99 -188 58 139 -24 -158 137 -244 -38 -1 135 -157 62 -40 68 70 6 224 62 -16 -93 -57 -214 54 -101 -15 17 152 -118 -315 -21 219 -135 127 216 357 -302 -87 -155 129 -26 -122 256 -319 -139 -62 14 62 22 84 -155 0 -52 0 -360 -50 -73 -50 -154 -90 -8 -231 272 -153 40 -189 -105 -146 -72 79 156 -46 -19 45 18 28 0 45 0 50 -50 57 -50 204 36 41 31 -213 -36 137 -43 -12 92 103 0 -181 0 -58 -50 -158 -50 0 94 -259 150 -33 -84 -17 -94 -13 -27 -101 -102 -85"""
+
+
+def side(key):
+    return PLACE.get(key, "s")
+
+
+def build():
+    O, AF = AluOpType, ActivationFunctionType
+    ops = []
+    cyc, pec = P["cyc"], P["pec"]
+
+    def v1(n): return max(64, n) * cyc
+    def vh(n): return max(64, n / 2) * cyc
+    def vg(n): return 0.055 + n * P["ga"] * cyc
+    def sg(n): return 0.07 + n * P["ga"] * cyc
+    tiny = v1(1)
+
+    def add(eng, cost, reads, writes, fn, name="", sem=None, n=1):
+        ops.append({"eng": eng, "cost": cost, "reads": reads, "writes": writes, "fn": fn, "name": name, "sem": sem, "n": n, "id": len(ops)})
+
+    def V(cost, reads, writes, fn, name=""): add("v", cost, reads, writes, fn, name)
+    def S(cost, reads, writes, fn, name=""): add("s", cost, reads, writes, fn, name)
+    def PE(cyc_n, reads, writes, fn, n, name=""): add("t", cyc_n * pec, reads, writes, fn, name, n=n)
+    def r(b, lo=0, hi=100000): return (b, lo, hi)
+
+    def ap(a):
+        if isinstance(a, (int, float)):
+            return lambda T: a
+        if isinstance(a, str):
+            return lambda T: T[a][:]
+        if len(a) == 3:
+            return lambda T: T[a[0]][:, a[1]:a[2]]
+        return lambda T: T[a[0]][:, a[1]:a[2]:a[3]]
+
+    def copy(out, in_): return lambda q, T: [q.tensor_copy(ap(out)(T), ap(in_)(T))]
+    def fill(out, x): return lambda q, T: [q.memset(ap(out)(T), x)]
+    def tt(out, a, b, op): return lambda q, T: [q.tensor_tensor(ap(out)(T), ap(a)(T), ap(b)(T), op)]
+    def scan(out, a, b, o0, o1): return lambda q, T: [q.tensor_tensor_scan(ap(out)(T), ap(a)(T), ap(b)(T), 0.0, o0, o1)]
+    def act(out, in_, f, **kw): return lambda q, T: [q.activation(ap(out)(T), ap(in_)(T), f, **dict((k, ap(x)(T)) for k, x in kw.items()))]
+
+    def ts(out, in0, s1, o1, s2=None, o2=None):
+        if o2 is None:
+            return lambda q, T: [q.tensor_scalar(ap(out)(T), ap(in0)(T), ap(s1)(T), None, o1)]
+        return lambda q, T: [q.tensor_scalar(ap(out)(T), ap(in0)(T), ap(s1)(T), ap(s2)(T), o1, o2)]
+
+    def gcopy(q_v, out, win, off):
+        if q_v:
+            return lambda q, T: [q.tensor_copy(ap(out)(T), ap(win)(T).indirect(ap(off)(T)))]
+        return lambda q, T: [q.activation(ap(out)(T), ap(win)(T).indirect(ap(off)(T)), AF.Copy)]
+
+    def gtt(out, win, off, b, op): return lambda q, T: [q.tensor_tensor(ap(out)(T), ap(win)(T).indirect(ap(off)(T)), ap(b)(T), op)]
+    def mm(out, terms): return lambda q, T: [q.matmul(ap(out)(T), ap(a)(T), ap(b)(T), i == 0, i == len(terms) - 1) for i, (a, b) in enumerate(terms)]
+
+    def either(key, nv, ns, reads, writes, fv, fs, name):
+        if side(key) == "v":
+            V(nv, reads, writes, fv, name)
+        else:
+            S(ns, reads, writes, fs, name)
+
+    def dma(eng, cost, reads, writes, sem, fn, k=1): add(eng, cost, reads, writes, fn, sem, sem=sem, n=k)
+    dma("y", 2.0, [], [r("TI")], "ldt", lambda q, T: [q.dma_start(T.TI[:], T.tube[:])])
+    dma("y", 2.0, [], [r("wi")], "ldw", lambda q, T: [q.dma_start(T.wi[:], T.wt[:])])
+    dma("y", 2.0, [], [r("ki")], "ldk", lambda q, T: [q.dma_start(T.ki[:], T.kn[:])])
+    dma("y", 2.0, [], [r("li")], "ldl", lambda q, T: [q.dma_start(T.li[:, 0:5], T.lim[:])])
+    dma("y", 9.0, [], [r("X", 0, 4096)], "ldx", lambda q, T: [q.dma_start(T.X[:, 0:4096], T.field[:, 0:4096])])
+    dma("s", 9.0, [], [r("X", 4096, 8192)], "ldy", lambda q, T: [q.dma_start(T.X[:, 4096:8192], T.field[:, 4096:8192])])
+    def G(cost, reads, writes, fn): add("g", cost, reads, writes, fn)
+    V(v1(64), [], [r("ones")], fill("ones", 1.0))
+    G(0.4, [], [r("pI")], lambda q, T: [q.iota(T.pI[:], [[0, 1]], 0, 1)])
+    G(0.4, [], [r("v1i")], lambda q, T: [q.iota(T.v1i[:], [[256, 8]], 0, 0)])
+    G(0.4, [], [r("v2i")], lambda q, T: [q.iota(T.v2i[:], [[16, 16]], -256, 0)])
+    G(0.4, [], [r("v3i")], lambda q, T: [q.iota(T.v3i[:], [[512, 16]], 0, 0)])
+    G(0.6, [], [r("irow")], lambda q, T: [q.iota(T.irow[:], [[0, 8], [1, 16]], 0, 0, allow_small_or_imprecise_dtypes=True)])
+    G(0.5, [r("ones")], [r("BO1")], lambda q, T: [q.affine_select(T.BO1[:], T.ones[:], [[-16, 8], [0, 16]], O.is_ge, 0.0, 0, 1)])
+    G(0.5, [r("BO1")], [r("BO")], lambda q, T: [q.affine_select(T.BO[:], T.BO1[:], [[16, 8], [0, 16]], O.is_ge, 0.0, 15, -1)])
+    G(0.5, [r("ones")], [r("IB")], lambda q, T: [q.affine_select(T.IB[:], T.ones[:], [[-1, 128]], O.is_equal, 0.0, 0, 1)])
+    V(v1(256), [r("TI")], [r("LU0")], copy("LU0", "TI"))
+    V(v1(1024), [], [r("RB")], fill("RB", 0.0))
+    V(v1(64), [r("RB")], [r("RB")], fill(("RB", 0, 1024, 16), 256.0))
+    V(tiny, [r("pI")], [r("iI")], ts("iI", "pI", 15, O.bitwise_and))
+    V(tiny, [r("iI")], [r("icol")], copy("icol", "iI"))
+    V(tiny, [r("wi")], [r("wc")], copy("wc", "wi"))
+    V(tiny, [r("ki")], [r("kc")], copy("kc", "ki"))
+    V(tiny, [r("li")], [r("lf")], copy(("lf", 0, 5), ("li", 0, 5)))
+    V(tiny, [r("lf")], [r("nl")], ts(("nl", 0, 5), ("lf", 0, 5), -1.0, O.mult, 0.5, O.add))
+    V(tiny, [r("nl")], [r("nth", 0, 1)], copy(("nth", 0, 1), ("nl", 0, 1)))
+    V(tiny, [r("lf")], [r("thv", 0, 1)], copy(("thv", 0, 1), ("lf", 0, 1)))
+    V(tiny, [r("icol")], [r("ige1")], ts("ige1", "icol", 1.0, O.is_ge))
+    V(tiny, [r("icol")], [r("e15")], ts("e15", "icol", 15.0, O.is_equal))
+    V(tiny, [r("ige1")], [r("pthr")], ts("pthr", "ige1", 102.0, O.mult, -101.0, O.add))
+    V(tiny, [r("ige1")], [r("pthv")], ts("pthv", "ige1", 109.5, O.mult, -101.0, O.add))
+    V(v1(1024), [], [r("sel")], fill("sel", 0.0))
+    for gg in range(8):
+        V(tiny, [r("BO")], [r("sel")], copy(("sel", 16 * gg, 16 * gg + 129 * 15 + 1, 129), ("BO", 16 * gg, 16 * gg + 16)))
+    V(tiny, [r("icol")], [r("i16")], ts("i16", "icol", 16.0, O.mult))
+    V(tiny, [r("i16"), r("v1i")], [r("VB")], ts("VB", "v1i", "i16", O.add))
+    V(vh(128), [r("BO"), r("wc")], [r("WB")], ts("WB", "BO", "wc", O.mult))
+    V(vh(128), [r("WB")], [r("WB256")], ts("WB256", "WB", 256.0, O.mult))
+    V(tiny, [], [r("c64", 0, 1)], lambda q, T: [q.memset(T.c64[0:32, :], -64.0)])
+    V(tiny, [], [r("c64", 1, 2)], lambda q, T: [q.memset(T.c64[32:64, :], 1.0 / 64)])
+    V(vh(128), [r("IB")], [r("nI")], ts("nI", "IB", -1.0, O.mult))
+    V(vh(128), [r("IB")], [r("n256I")], ts("n256I", "IB", -256.0, O.mult))
+    V(v1(128), [r("IB")], [r("IF")], copy("IF", "IB"))
+    V(tiny, [r("kc")], [r("k2")], ts("k2", "kc", -256.0, O.add))
+    V(tiny, [r("k2")], [r("sqb")], ts("sqb", "k2", 2.0, O.mult))
+    V(tiny, [r("k2")], [r("k3")], ts("k3", "k2", "k2", O.mult, -4.0, O.mult))
+    V(tiny, [r("k3")], [r("k4")], ts("k4", "k3", -0.25, O.add))
+    V(v1(2048), [], [r("ZS")], fill("ZS", 0.0))
+    V(v1(512), [], [r("R01")], fill("R01", 1.0))
+    V(v1(64), [r("R01")], [r("R01")], fill(("R01", 0, 1024, 16), 0.0))
+    V(vh(2048), [r("sel")], [r("sel256")], ts("sel256", "sel", 256.0, O.mult))
+    V(tiny, [r("icol"), r("v2i")], [r("VW")], ts("VW", "v2i", "icol", O.add))
+    V(tiny, [r("BO")], [r("blk32")], ts("blk32", ("BO", 0, 128, 16), 32.0, O.mult))
+    V(tiny, [r("BO")], [r("blkn")], ts("blkn", ("BO", 0, 128, 16), -16.0, O.mult))
+    V(v1(64), [], [r("RK")], fill("RK", 0.0))
+    V(tiny, [r("RK")], [r("RK")], fill(("RK", 0, 128, 16), 1048576.0))
+    for c in range(2):
+        V(v1(128), [], [r("KS%d" % c)], fill("KS%d" % c, 0.0))
+    V(vh(128), [r("IB"), r("ige1")], [r("pIm")], ts("pIm", "IB", "ige1", O.mult))
+    V(vh(128), [r("pIm")], [r("nIm")], ts("nIm", "pIm", -1.0, O.mult))
+    V(v1(128), [r("sel")], [r("Sel0")], copy("Sel0", ("sel", 0, 128)))
+    V(vh(2048), [r("sel"), r("icol")], [r("isel")], ts("isel", "sel", "icol", O.mult))
+    V(vh(2048), [r("sel"), r("wc")], [r("wsel")], ts("wsel", "sel", "wc", O.mult))
+    V(tiny, [r("icol")], [r("i32c")], ts("i32c", "icol", 32.0, O.mult))
+    V(tiny, [r("v3i"), r("i32c")], [r("SOp")], ts("SOp", "v3i", "i32c", O.add))
+    V(v1(64), [], [r("half")], fill("half", 0.5))
+    V(vh(128), [r("ones"), r("e15")], [r("S15")], ts("S15", "ones", "e15", O.mult))
+    for c in range(2):
+        S(v1(2048), [r("ZS")], [r("W", 2048 * c, 2048 * c + 2048)], act(("W", 2048 * c, 2048 * c + 2048), ("ZS", 2048 * c, 2048 * c + 2048), AF.Copy))
+
+    C35 = 1.5 * 2.0 ** 35
+    C24 = 1.5 * 2.0 ** 24
+    nsel = [("sel", 128 * k, 128 * k + 128) for k in range(16)]
+    for t in range(RO):
+        last = t == RO - 1
+        LU, NU = "LU%d" % t, "NU%d" % t
+        if t:
+            for c, (a0, n, pcs) in enumerate(CHUNKS):
+                add("x", P["hop"], [r("NU%d" % (t - 1), a0, a0 + n)], [r(LU, a0, a0 + n)], None, "arr", sem="arr%d%d" % (t, c))
+        for c, (a0, n, pcs) in enumerate(CHUNKS):
+            a1 = a0 + n
+            V(v1(n), [r(LU, a0, a1)], [r("L32", a0, a1)], copy(("L32", a0, a1), (LU, a0, a1)), "L32 c%d t%d" % (c, t))
+            S(v1(n), [r("L32", a0, a1), r("k4")], [r("LQ", a0, a1)], act(("LQ", a0, a1), ("L32", a0, a1), AF.Identity, bias="k4"), "LQ c%d t%d" % (c, t))
+        dma("y", 2.0, [r("L32")], [r("DL")], "dl", lambda q, T: [q.dma_start(T.DL[:], T.L32[:])])
+        dma("y", P["wdma"], [r("DL")], [r("W")], "w", lambda q, T: [q.dma_start(T.W[j::16, 256 * j:4096], T.DL[:, 1:17 - j, :]) for j in range(1, 16)], 15)
+        for c, (a0, n, pcs) in enumerate(CHUNKS):
+            c0, b0 = 16 * a0, "pb%d0" % (c % 2)
+            for p, (p0, pn) in enumerate(pcs):
+                lo, hi, m = c0 + 16 * p0, c0 + 16 * (p0 + pn), 16 * pn
+                u0, u1 = a0 + p0, a0 + p0 + pn
+                key = "c%d s%d" % (c, p)
+                pt = " %s t%d" % (key, t)
+                either("G " + key, vg(m), sg(m), [r("X"), r(LU, u0, u1)], [r("G", lo, hi)],
+                       gcopy(True, ("G", lo, hi), ("X", 0, 8192), (LU, u0, u1)), gcopy(False, ("G", lo, hi), ("X", 0, 8192), (LU, u0, u1)), "G" + pt)
+                V(vh(m), [r("G", lo, hi), r("RB")], [r("M", lo, hi)], scan(("M", lo, hi), ("RB", 0, m), ("G", lo, hi), O.max, O.min), "M" + pt)
+            for k in range(n // UNIT):
+                lo, hi, m = c0 + 16 * UNIT * k, c0 + 16 * UNIT * (k + 1), 16 * UNIT
+                u0, u1 = a0 + UNIT * k, a0 + UNIT * (k + 1)
+                key = "c%d u%d" % (c, k)
+                ut = " %s t%d" % (key, t)
+                if side("I " + key) == "s":
+                    S(v1(m), [r("M", lo, hi), r("nth", t, t + 1)], [r("H", lo, hi)], act(("H", lo, hi), ("M", lo, hi), AF.Sign, bias=("nth", t, t + 1)), "I" + ut)
+                    th = "pthr"
+                else:
+                    V(vh(m), [r("M", lo, hi), r("thv", t, t + 1)], [r("H", lo, hi)], ts(("H", lo, hi), ("M", lo, hi), ("thv", t, t + 1), O.is_ge), "I" + ut)
+                    th = "pthv"
+                cn = (b0, UNIT * k, UNIT * (k + 1))
+                PE(64 * 16, [r("H", lo, hi), r("sel")], [r(*cn)], mm(cn, [(nsel[j], ("H", lo + j, hi, 16)) for j in range(16)]), 16, "cnt" + ut)
+                V(v1(UNIT), [r(*cn), r(th)], [r("pas", u0, u1)], ts(("pas", u0, u1), cn, th, O.is_ge), "pass" + ut)
+        nwt = ("pb11", 256, 272)
+        PE(64 * 17, [r("pas"), r("sel256"), r("IB"), r("VW")], [r(*nwt)],
+           mm(nwt, [("IB", "VW")] + [(("sel256", 128 * k, 128 * k + 128), ("pas", k, 256, 16)) for k in range(16)]), 17, "nw t%d" % t)
+        V(tiny, [r(*nwt)], [r("OW")], copy("OW", nwt), "OW t%d" % t)
+        V(vg(256), [r("W"), r("OW"), r("pas")], [r("R1")], gtt("R1", ("W", 0, 4096), "OW", "pas", O.mult), "R1 t%d" % t)
+        for k in range(2):
+            npk = ("pk0", 256 + 128 * k, 384 + 128 * k)
+            PE(256, [r("pas"), r("pIm"), r("nIm"), r("ones")], [r(*npk)], mm(npk, [("pIm", "ones"), ("nIm", ("pas", 128 * k, 128 * k + 128))]), 2, "np t%d" % t)
+        for c, (a0, n, pcs) in enumerate(CHUNKS):
+            a1, c0, c1, h0, h1 = a0 + n, 16 * a0, 16 * (a0 + n), a0 // 16, (a0 + n) // 16
+            b = c % 2
+            b0, b1, b2, pk = "pb%d0" % b, "pb%d1" % b, "pb%d2" % b, "pk%d" % b
+            tag = " c%d t%d" % (c, t)
+            R = lambda x, a0=a0, a1=a1: r(x, a0, a1)
+            Q = lambda x, a0=a0, a1=a1: (x, a0, a1)
+            W = lambda x, c0=c0, c1=c1: r(x, c0, c1)
+            nbt = (b0, 128, 128 + n // 16)
+            PE(64 * 17, [R("pas"), r("sel"), r("IB"), r("VB")], [r(*nbt)],
+               mm(nbt, [("IB", ("VB", 0, n // 16))] + [(nsel[k], ("pas", a0 + k, a1, 16)) for k in range(16)]), 17, "nb" + tag)
+            V(tiny, [r(*nbt)], [r("OM", h0, h1)], ts(("OM", h0, h1), nbt, -1.0, O.add), "OM" + tag)
+            either("XL c%d" % c, vg(n), sg(n), [W("G"), r("OM", h0, h1)], [R("XL")],
+                   gcopy(True, Q("XL"), ("G", c0, c1), ("OM", h0, h1)), gcopy(False, Q("XL"), ("G", c0, c1), ("OM", h0, h1)), "XL" + tag)
+            zs = ("ZS", c0, c1, 16)
+            either("Z c%d" % c, vg(n), sg(n), [W("M"), r("OM", h0, h1)], [W("ZS")],
+                   gcopy(True, zs, ("M", c0, c1), ("OM", h0, h1)), gcopy(False, zs, ("M", c0, c1), ("OM", h0, h1)), "Z" + tag)
+            s_, u_, q_ = (b0, 256, 256 + n), (b1, 0, n), (b2, 0, n)
+            PE(2 * n, [R("XL"), r("WB"), r("ones"), r("c64")], [r(*s_)],
+               lambda q, T, s_=s_, n=n, x=Q("XL"): [q.matmul(ap(s_)(T), T.ones[0:64, :], T.c64[:, 0:n], True, False), q.matmul(ap(s_)(T), T.WB[:], ap(x)(T), False, True)], 2, "s" + tag)
+            V(v1(n), [r(*s_)], [R("B4")], ts(Q("B4"), s_, C35, O.add, -C35, O.add), "B4" + tag)
+            PE(2 * n, [R("XL"), r("WB"), r("nI"), R("B4")], [r(*u_)], mm(u_, [("WB", Q("XL")), ("nI", Q("B4"))]), 2, "u" + tag)
+            S(v1(n), [r(*u_), r("sqb")], [R("SQ")], act(Q("SQ"), u_, AF.Square, bias="sqb", scale=0.25), "SQ" + tag)
+            PE(6 * n, [R("XL"), r("WB256"), r("n256I"), R("B4"), r("IF"), R("LQ")], [r(*q_)],
+               mm(q_, [("WB256", Q("XL")), ("n256I", Q("B4")), ("IF", Q("LQ"))]), 3, "q" + tag)
+            V(v1(n), [r(*q_), R("SQ")], [R("xI")], tt(Q("xI"), q_, Q("SQ"), O.add), "x" + tag)
+            V(v1(n), [R("xI")], [R("cI")], ts(Q("cI"), Q("xI"), 8191, O.bitwise_and), "and" + tag)
+            V(v1(n), [R("cI")], [R("CU")], copy(Q("CU"), Q("cI")), "CU" + tag)
+            modes = []
+            for p, (p0, pn) in enumerate(pcs):
+                lo, hi, m = c0 + 16 * p0, c0 + 16 * (p0 + pn), 16 * pn
+                u0, u1 = a0 + p0, a0 + p0 + pn
+                key = "c%d s%d" % (c, p)
+                pt = " %s t%d" % (key, t)
+                D, A, z16, d16, sv = ("D", lo, hi), ("A", lo, hi), ("ZS", lo, hi, 16), ("D", lo, hi, 16), ("sv", u0, u1)
+                V(vh(m), [r("ZS", lo, hi), r("R01")], [r("Zx", lo, hi)], scan(("Zx", lo, hi), ("R01", 0, m), ("ZS", lo, hi), O.mult, O.add), "Zx" + pt)
+                modes.append(side("C " + key))
+                if modes[-1] == "v":
+                    V(vg(m), [r("X"), r("CU", u0, u1), r("Zx", lo, hi)], [r(*D)], gtt(D, ("X", 0, 8192), ("CU", u0, u1), ("Zx", lo, hi), O.subtract), "D" + pt)
+                    either("A " + key, vh(m), v1(m), [r(*D)], [r(*A)], ts(A, D, 0.0, O.max), act(A, D, AF.Relu), "A" + pt)
+                else:
+                    S(sg(m), [r("X"), r("CU", u0, u1)], [r(*D)], gcopy(False, D, ("X", 0, 8192), ("CU", u0, u1)), "D" + pt)
+                    S(v1(pn), [r(*D)], [r(*sv)], act(sv, d16, AF.Copy), "sv" + pt)
+                    V(v1(2 * pn), [r(*D), r("ZS", lo, hi), r(*sv)], [r(*D)], tt(d16, sv, z16, O.max), "fx" + pt)
+                    V(vh(m), [r(*D), r("Zx", lo, hi)], [r(*A)], scan(A, ("Zx", lo, hi), D, O.min, O.max), "A" + pt)
+                    S(v1(pn), [r(*sv), r(*A)], [r(*D)], act(d16, sv, AF.Copy), "rs" + pt)
+                if not last:
+                    f = 2.0 if modes[-1] == "v" else 1.0
+                    either("Z2 " + key, v1(pn), v1(pn), [r("ZS", lo, hi)], [r("Z2", u0, u1)],
+                           ts(("Z2", u0, u1), z16, f, O.mult, -0.5, O.add), act(("Z2", u0, u1), z16, AF.Copy, bias=-0.5, scale=f), "Z2" + pt)
+
+            def keyhalf(first, x, y, c0=c0, c1=c1, n=n, pk=pk):
+                def f(q, T):
+                    o = [q.matmul(T[pk][0:n, 0:128], T.ones[0:1, 0:n], T.irow[:], True, False)] if first else []
+                    return o + [q.matmul(T[pk][0:n, i:128:16], T[x][:, c0 + i:c1:16], T[y][:], False, not first and i == 15) for i in range(16)]
+                return f
+            hs = [("D", "blkn"), ("A", "blk32")]
+            if "s" in modes:
+                hs.reverse()
+            for k, (x, y) in enumerate(hs):
+                PE(64 * 16 + 128 * (1 - k), [W(x), r(y), r("irow"), r("ones")] + [r(pk, 0, 128)] * k, [r(pk, 0, 128)], keyhalf(k == 0, x, y), 17 - k, "key%d" % k + tag)
+            KM, KS, KB, OH = "KM%d" % b, "KS%d" % b, "KB%d" % b, "OH%d" % b
+
+            def rows(x, lo=0, hi=128, st=1, n=n): return lambda T: T[x][0:n, lo:hi:st] if st > 1 else T[x][0:n, lo:hi]
+            V(v1(128), [r(pk, 0, 128), r("RK")], [r(KM)], lambda q, T, n=n, KM=KM, pk=pk: [q.tensor_tensor_scan(T[KM][0:n, :], T.RK[0:n, :], T[pk][0:n, 0:128], 0.0, O.max, O.min)], "KM" + tag)
+            V(tiny, [r(KM)], [r(KS)], lambda q, T, n=n, KM=KM, KS=KS: [q.tensor_copy(T[KS][0:n, ::16], T[KM][0:n, 15::16])], "KS" + tag)
+            V(v1(128), [r(KS), r("R01")], [r(KB)], lambda q, T, n=n, KS=KS, KB=KB: [q.tensor_tensor_scan(T[KB][0:n, :], T.R01[0:n, 0:128], T[KS][0:n, :], 0.0, O.mult, O.add)], "KB" + tag)
+            V(v1(128), [r(pk, 0, 128), r(KB)], [r(OH)], lambda q, T, n=n, KB=KB, pk=pk, OH=OH: [q.tensor_tensor(T[OH][0:n, :], T[pk][0:n, 0:128], T[KB][0:n, :], O.is_equal)], "OH" + tag)
+            oh = (b0, 384, 384 + n)
+            PE(n, [r(OH), r("IB")], [r(*oh)], lambda q, T, n=n, OH=OH, oh=oh: [q.matmul(ap(oh)(T), T[OH][0:n, :], T.IB[0:n, 0:n], True, True)], 1, "OHA" + tag)
+            if not last:
+                either("OHA c%d" % c, v1(n), v1(n), [r(*oh)], [R("OHA")], copy(Q("OHA"), oh), act(Q("OHA"), oh, AF.Copy), "OHAe" + tag)
+                tot = (b1, 128, 128 + n // 16)
+                PE(64 * 17, [R("OHA"), r("isel"), r("IB"), r("VB")], [r(*tot)],
+                   mm(tot, [("IB", ("VB", 0, n // 16))] + [(("isel", 128 * k, 128 * k + 128), ("OHA", a0 + k, a1, 16)) for k in range(16)]), 17, "to" + tag)
+                V(tiny, [r(*tot)], [r("OT", h0, h1)], copy(("OT", h0, h1), tot), "OT" + tag)
+                V(vg(n), [W("D"), r("OT", h0, h1), R("Z2")], [R("tt")], gtt(Q("tt"), ("D", c0, c1), ("OT", h0, h1), Q("Z2"), O.add), "tt" + tag)
+                V(v1(n), [R("tt")], [R("Y2")], ts(Q("Y2"), Q("tt"), C24, O.add, -C24, O.add), "Y2" + tag)
+            np_, nl_ = ("pk0", 256 + a0, 256 + a1), (b2, 256, 256 + n)
+            V(v1(n), [r(*np_), R("cI")], [R("C1")], tt(Q("C1"), np_, Q("cI"), O.mult), "C1" + tag)
+            V(v1(n), [r(*oh), R("cI")], [R("OC")], tt(Q("OC"), oh, Q("cI"), O.mult), "OC" + tag)
+            PE(12 * n, [R("R1"), R("C1"), R("OC"), r("IF"), r("Sel0")], [r(*nl_)], mm(nl_, [("IF", Q("R1")), ("IF", Q("C1")), ("Sel0", Q("OC"))]), 3, "nl" + tag)
+            if not last:
+                V(v1(n), [r(*nl_)], [R(NU)], copy(Q(NU), nl_), "NU" + tag)
+                add("g", 0.5, [R(NU)], [], ("send", t, c), "send" + tag, sem="sent")
+            else:
+                S(v1(n), [r(*nl_)], [R("yls")], act(Q("yls"), nl_, AF.Copy), "yls" + tag)
+                dma("y", 2.0, [R("yls")], [], "ol%d" % c, lambda q, T, x=Q("yl"), y=Q("yls"): [q.dma_start(ap(x)(T), ap(y)(T))])
+                S(v1(n), [W("ZS")], [R("yzs")], act(Q("yzs"), zs, AF.Copy), "yzs" + tag)
+                dma("y", 2.0, [R("yzs")], [], "oz%d" % c, lambda q, T, x=Q("yz"), y=Q("yzs"): [q.dma_start(ap(x)(T), ap(y)(T))])
+        if not last:
+            tag = " t%d" % t
+            sb = ("pb11", 144, 160)
+            PE(64 * 16, [r("XL"), r("wsel")], [r(*sb)], mm(sb, [(("wsel", 128 * k, 128 * k + 128), ("XL", k, 256, 16)) for k in range(16)]), 16, "sb" + tag)
+            V(tiny, [r(*sb)], [r("soA")], copy("soA", sb), "soA" + tag)
+            V(tiny, [r("soA")], [r("soB")], ts("soB", "soA", 31, O.bitwise_and), "soB" + tag)
+            V(tiny, [r("soB"), r("SOp")], [r("soC")], tt("soC", "soB", "SOp", O.add), "soC" + tag)
+            V(tiny, [r("soC")], [r("SO")], copy("SO", "soC"), "SO" + tag)
+            eb = ("pb11", 192, 256)
+            PE(64 * 4, [r("pas"), r("S15")], [r(*eb)], mm(eb, [("S15", ("pas", 64 * k, 64 * k + 64)) for k in range(4)]), 4, "E" + tag)
+            V(tiny, [r(*eb)], [r("er")], lambda q, T: [q.tensor_reduce(T.er[:], T.pb11[:, 192:256], AxisListType.X, O.add, negate=True)], "er" + tag)
+            V(tiny, [r("er")], [r("eI")], copy("eI", "er"), "eI" + tag)
+            V(tiny, [r("eI")], [r("eJ")], ts("eJ", "eI", 7, O.bitwise_and), "eJ" + tag)
+            n1 = (t + 1, t + 2)
+            who = [side("I c%d u%d" % (c, k)) for c, (a0, n, pcs) in enumerate(CHUNKS) for k in range(n // UNIT)]
+            if "s" in who:
+                V(tiny, [r("eJ"), r("nl")], [r("nth", *n1)], tt(("nth",) + n1, ("nl",) + n1, "eJ", O.subtract), "nth" + tag)
+            if "v" in who:
+                V(tiny, [r("eJ"), r("lf")], [r("thv", *n1)], tt(("thv",) + n1, ("lf",) + n1, "eJ", O.add), "thv" + tag)
+            for c, (a0, n, pcs) in enumerate(CHUNKS):
+                h0, h1 = a0 // 16, (a0 + n) // 16
+                V(0.055 + 3.5 * n * cyc, [r("Y2", a0, a0 + n), r("half"), r("SO")], [r("X")],
+                  lambda q, T, y=("Y2", a0, a0 + n), h=("half", 0, n), o=("SO", h0, h1): [q.tensor_tensor(T.X[:, 0:8192].indirect(ap(o)(T)), ap(y)(T), ap(h)(T), O.mult)], "scat c%d" % c + tag)
+    return ops
+
+
+def deps_of(ops):
+    acc = {}
+    for o in ops:
+        d = set()
+        for (b, lo, hi) in o["reads"]:
+            for (p, l2, h2, w) in acc.get(b, []):
+                if w and l2 < hi and lo < h2:
+                    d.add((p, "raw"))
+        for (b, lo, hi) in o["writes"]:
+            for (p, l2, h2, w) in acc.get(b, []):
+                if l2 < hi and lo < h2:
+                    d.add((p, "waw" if w else "war"))
+        for (b, lo, hi) in o["writes"]:
+            acc[b] = [a for a in acc.get(b, []) if not (lo <= a[1] and a[2] <= hi)] + [(o["id"], lo, hi, True)]
+        for (b, lo, hi) in o["reads"]:
+            acc.setdefault(b, []).append((o["id"], lo, hi, False))
+        o["deps"] = sorted((p, k) for (p, k) in d if p != o["id"])
+        o["banks"] = sorted(set(b for (b, lo, hi) in o["reads"] + o["writes"] if b.startswith("pb") or b.startswith("pk")))
+    return ops
+
+
+def schedule(ops):
+    n = len(ops)
+    wake = P["wake"]
+    succ = [[] for _ in range(n)]
+    left = [0] * n
+    for o in ops:
+        ps = set(p for (p, k) in o["deps"])
+        left[o["id"]] = len(ps)
+        for p in ps:
+            succ[p].append(o["id"])
+    prio = [0.0] * n
+    for o in reversed(ops):
+        prio[o["id"]] = o["cost"] + max([prio[s] + wake for s in succ[o["id"]]], default=0.0) + PRI.get(o["name"].rsplit(" t", 1)[0], 0.0)
+    fin = [0.0] * n
+    start = [0.0] * n
+    avail = [0.0] * n
+    free = {"x": 0.0}
+    bank = {}
+    ready = [o["id"] for o in ops if left[o["id"]] == 0]
+    order = []
+    while ready:
+        cand = []
+        first = 1e9
+        for i in ready:
+            o = ops[i]
+            e = o["eng"]
+            st = max(avail[i], free.get(e, 0.0))
+            for b in o["banks"]:
+                for e2, f2 in bank.get(b, {}).items():
+                    if e2 != e and f2 + wake > st:
+                        st = f2 + wake
+            cand.append((st, -prio[i], i))
+            if st < first:
+                first = st
+        pr, st, i = min((p, s, j) for (s, p, j) in cand if s <= first + 0.03)
+        o = ops[i]
+        e = o["eng"]
+        start[i] = st
+        fin[i] = st + o["cost"]
+        if o["sem"] and e in ("y", "s"):
+            free[e] = st + 0.06 * o["n"]
+        elif e != "x":
+            free[e] = fin[i]
+        for b in o["banks"]:
+            bank.setdefault(b, {})[e] = fin[i]
+        order.append(i)
+        ready.remove(i)
+        for s in succ[i]:
+            left[s] -= 1
+            if left[s] == 0:
+                ready.append(s)
+                a = 0.0
+                for (p, k) in ops[s]["deps"]:
+                    if not (k == "war" and ops[p]["eng"] == ops[s]["eng"]):
+                        a = max(a, fin[p] + wake)
+                avail[s] = a
+    return order, start, fin
+
+
+def free_steps():
+    out = []
+    for c, (a0, n, pcs) in enumerate(CHUNKS):
+        for p in range(len(pcs)):
+            out += ["%s c%d s%d" % (x, c, p) for x in ("G", "C", "A", "Z2")]
+        out += ["I c%d u%d" % (c, k) for k in range(n // UNIT)] + ["%s c%d" % (x, c) for x in ("Z", "XL", "OHA")]
+    return out
+
+
+def step_names():
+    keep, names = dict(PLACE), set()
+    for e in "sv":
+        for k in free_steps():
+            PLACE[k] = e
+        names |= set(o["name"].rsplit(" t", 1)[0] for o in build() if " t" in o["name"])
+    PLACE.clear()
+    PLACE.update(keep)
+    return sorted(names)
+
+
+PLACE.update(zip(free_steps(), SIDES))
+PRI.update((k, int(x) / 10) for k, x in zip(step_names(), RANKS.split()))
+
+
+def rank_program(g, core, T, topo):
+    rank = T.rank_of(core)
+    if rank is None:
+        return
+    cores = T.cores
+    dst = cores[(rank + 1) % len(cores)]
+    rid, pid, _ = topo.addr(dst)
+    mask = topo.mask(core, dst)
+    ne = len(topo.engines(core, dst))
+    ni = len(topo.engines(cores[(rank - 1) % len(cores)], core))
+    ops = deps_of(build())
+    order = schedule(ops)[0]
+    queues = {"v": g.vector, "s": g.scalar, "t": g.tensor, "g": g, "y": g.sync}
+    csem = {"v": "cv", "s": "cs", "t": "ct", "g": "cg"}
+    total = {}
+    token = {}
+    after = {}
+    know = {e: {} for e in queues}
+    lastbank = {}
+    for i in order:
+        o = ops[i]
+        e = o["eng"]
+        if e == "x":
+            token[i] = (o["sem"], ni)
+            total[o["sem"]] = ni
+            after[i] = {}
+            continue
+        q = queues[e]
+        need = {}
+        ds = [p for (p, k) in o["deps"] if not (k == "war" and ops[p]["eng"] == e and token[p][0] == csem.get(e))]
+        if e == "t":
+            ds = [p for p in ds if ops[p]["eng"] != "t"]
+        for b in o["banks"]:
+            for e2, p in lastbank.get(b, {}).items():
+                if e2 != e:
+                    ds.append(p)
+        inherit = []
+        for p in ds:
+            s, v = token[p]
+            if know[e].get(s, 0) < v:
+                need[s] = max(need.get(s, 0), v)
+                inherit.append(p)
+        for s in sorted(need):
+            if any(after[p].get(s, 0) >= need[s] and token[p][0] != s for p in inherit):
+                continue
+            q.wait_ge(T.sem[s], int(need[s]))
+        for p in inherit:
+            s, v = token[p]
+            for s2, v2 in list(after[p].items()) + [(s, v)]:
+                if know[e].get(s2, 0) < v2:
+                    know[e][s2] = v2
+        after[i] = dict(know[e])
+        if isinstance(o["fn"], tuple):
+            _, t, c = o["fn"]
+            a0, n, _ = CHUNKS[c]
+            g.remote_dma(T["LU%d" % (t + 1)][:, a0:a0 + n], T["NU%d" % t][:, a0:a0 + n], T.sem["arr%d%d" % (t + 1, c)], T.sem["sent"], pid, rid, mask)
+            total["sent"] = total.get("sent", 0) + ne
+            token[i] = ("sent", total["sent"])
+        else:
+            ins = o["fn"](q, T)
+            s, k = (o["sem"], 16) if o["sem"] else (csem[e], 1)
+            for x in ins:
+                x.then_inc(T.sem[s], k)
+            total[s] = total.get(s, 0) + k * len(ins)
+            token[i] = (s, total[s])
+        for b in o["banks"]:
+            lastbank.setdefault(b, {})[e] = i
+    for s in sorted(total):
+        g.wait_ge(T.sem[s], int(total[s]))

@@ -5,7 +5,7 @@ CHUNKS = [(0, 128, [(0, 32), (32, 32), (64, 32), (96, 32)]), (128, 128, [(0, 32)
 UNIT = 64
 
 BF, F32, I32, U16 = "bfloat16", "float32", "int32", "uint16"
-SCRATCH = {"DL": ("dram", [8, 16, 256], F32), "irow": ("sbuf", [1, 128], BF), "c64": ("sbuf", [64, 128], BF)}
+SCRATCH = {"DL0": ("dram", [8, 16, 128], F32), "DL1": ("dram", [8, 16, 128], F32), "irow": ("sbuf", [1, 128], BF), "grow": ("sbuf", [1, 128], BF), "c64": ("sbuf", [64, 128], BF)}
 for _n, _w, _d in (
         ("X", 8192, BF), ("TI", 256, I32), ("wi", 1, I32), ("ki", 1, I32), ("li", 8, I32),
         ("wc", 1, F32), ("kc", 1, F32), ("nl", 8, F32), ("lf", 8, F32), ("k2", 1, F32), ("k3", 1, F32), ("k4", 1, F32), ("sqb", 1, F32),
@@ -14,7 +14,7 @@ for _n, _w, _d in (
         ("ones", 128, BF), ("BO1", 128, BF), ("BO", 128, BF), ("IB", 128, BF), ("IF", 128, F32),
         ("nI", 128, BF), ("n256I", 128, BF), ("pIm", 128, BF), ("nIm", 128, BF), ("WB", 128, BF), ("WB256", 128, BF),
         ("S15", 128, BF), ("Sel0", 128, F32), ("LQ", 256, F32),
-        ("sel", 2048, BF), ("isel", 2048, BF), ("wsel", 2048, BF), ("sel256", 2048, BF), ("blk32", 8, BF), ("blkn", 8, BF),
+        ("sel", 2048, BF), ("isel", 2048, BF), ("wsel", 2048, BF), ("sel128", 2048, BF), ("blk32", 8, BF), ("blk16", 8, BF), ("blkn", 8, BF),
         ("v1i", 8, I32), ("v2i", 16, I32), ("v3i", 16, I32), ("VB", 8, BF), ("VW", 16, BF), ("SOp", 16, I32),
         ("R01", 1024, BF), ("RB", 1024, BF), ("RK", 128, BF), ("half", 128, BF), ("W", 4096, F32),
         ("soA", 16, I32), ("soB", 16, I32), ("soC", 16, I32), ("SO", 16, U16),
@@ -25,8 +25,8 @@ for _n, _w, _d in (
         ("OC", 256, F32), ("C1", 256, F32), ("R1", 256, F32), ("tt", 256, F32), ("Y2", 256, BF), ("yls", 256, F32), ("yzs", 256, F32)):
     SCRATCH[_n] = ("sbuf", [128, _w], _d)
 for _c in range(2):
-    for _b in ("KM", "KS", "KB"):
-        SCRATCH["%s%d" % (_b, _c)] = ("sbuf", [128, 128], F32)
+    SCRATCH["KM%d" % _c] = ("sbuf", [128, 144], F32)
+    SCRATCH["KB%d" % _c] = ("sbuf", [128, 128], F32)
     SCRATCH["OH%d" % _c] = ("sbuf", [128, 128], BF)
     for _b in ("pb%d0", "pb%d1", "pb%d2", "pk%d"):
         SCRATCH[_b % _c] = ("psum", [128, 512], F32)
@@ -35,14 +35,14 @@ for _t in range(RO):
     if _t < RO - 1:
         SCRATCH["NU%d" % _t] = ("sbuf", [128, 256], U16)
 
-SEMAPHORES = ["cv", "cs", "ct", "cg", "sent", "ldt", "ldw", "ldk", "ldl", "ldx", "ldy", "dl", "w"] + \
-    ["%s%d" % (a, c) for a in ("oz", "ol") for c in range(len(CHUNKS))] + ["arr%d%d" % (t, c) for t in range(1, RO) for c in range(len(CHUNKS))]
+SEMAPHORES = ["cv", "cs", "ct", "cg", "sent", "ldt", "ldw", "ldk", "ldl", "ldx", "ldy"] + \
+    ["%s%d" % (a, c) for a in ("oz", "ol", "dl", "w") for c in range(len(CHUNKS))] + ["arr%d%d" % (t, c) for t in range(1, RO) for c in range(len(CHUNKS))]
 
-P = {"cyc": 0.83e-3 * 1.2, "ga": 1.6, "pec": 0.417e-3 * 1.2, "wake": 0.06, "hop": 3.5, "wdma": 6.0}
+P = {"cyc": 0.92e-3, "ga": 1.56, "pec": 0.5e-3, "wake": 0.18, "hop": 5.0, "wdma": 7.0}
 PLACE = {}
 PRI = {}
-SIDES = "ssvsvvssssvsssssvsssvssssvvssssvvvssvsssvs"
-RANKS = """-348 -185 -40 78 -145 -186 -27 51 -54 -95 -114 108 93 -40 -323 100 -160 -231 -37 -244 -97 147 -103 123 -188 121 77 -166 -10 -17 70 13 85 -23 -38 -23 199 35 -22 244 35 -10 169 -114 -234 25 -153 -163 -7 -79 -139 17 47 99 -188 58 139 -24 -158 137 -244 -38 -1 135 -157 62 -40 68 70 6 224 62 -16 -93 -57 -214 54 -101 -15 17 152 -118 -315 -21 219 -135 127 216 357 -302 -87 -155 129 -26 -122 256 -319 -139 -62 14 62 22 84 -155 0 -52 0 -360 -50 -73 -50 -154 -90 -8 -231 272 -153 40 -189 -105 -146 -72 79 156 -46 -19 45 18 28 0 45 0 50 -50 57 -50 204 36 41 31 -213 -36 137 -43 -12 92 103 0 -181 0 -58 -50 -158 -50 0 94 -259 150 -33 -84 -17 -94 -13 -27 -101 -102 -85"""
+SIDES = "ssvvvvssssssvssvvvvvssssvsvssssvvsvsssvvvs"
+RANKS = """-1053 350 636 58 307 -417 24 7 554 899 142 -285 -395 -437 -1677 -149 -409 -436 619 26 -740 333 -133 1078 405 2415 673 -982 -837 780 544 -708 -54 748 -40 -413 196 258 1 -876 -251 -104 -441 474 596 -22 613 800 -1231 215 -680 921 -14 411 660 -882 -439 50 -312 -84 38 146 -475 155 819 809 -182 -282 -30 467 314 338 789 105 -183 -60 1085 -31 -199 26 -394 -338 -98 -157 -236 -574 226 -543 -558 357 -75 -794 -247 250 -135 -377 -1804 69 -1492 -374 204 -943 506 -52 490 -134 484 108 576 -343 472 -216 153 535 -47 222 -1072 -619 -451 287 -607 -55 -304 210 259 -248 788 -831 -855 890 45 -490 229 -561 -601 155 741 295 -332 -60 -228 -596 -328 323 -344 60 -556 279 -181 -33 -271 -238 -385 -553 -508 357 -869 -66 -5 -410 932 374 520 502 202 -52 -1367 -146"""
 
 
 def side(key):
@@ -113,9 +113,11 @@ def build():
     V(v1(64), [], [r("ones")], fill("ones", 1.0))
     G(0.4, [], [r("pI")], lambda q, T: [q.iota(T.pI[:], [[0, 1]], 0, 1)])
     G(0.4, [], [r("v1i")], lambda q, T: [q.iota(T.v1i[:], [[256, 8]], 0, 0)])
-    G(0.4, [], [r("v2i")], lambda q, T: [q.iota(T.v2i[:], [[16, 16]], -256, 0)])
+    G(0.4, [], [r("v2i")], lambda q, T: [q.iota(T.v2i[:], [[0, 2], [16, 8]], -128, 0)])
     G(0.4, [], [r("v3i")], lambda q, T: [q.iota(T.v3i[:], [[512, 16]], 0, 0)])
     G(0.6, [], [r("irow")], lambda q, T: [q.iota(T.irow[:], [[0, 8], [1, 16]], 0, 0, allow_small_or_imprecise_dtypes=True)])
+    G(0.6, [], [r("grow")], lambda q, T: [q.iota(T.grow[:], [[16384, 8], [0, 16]], 0, 0, allow_small_or_imprecise_dtypes=True)])
+    V(tiny, [r("grow")], [r("grow")], lambda q, T: [q.tensor_scalar(T.grow[:], T.grow[:], 16.0, None, O.mult)])
     G(0.5, [r("ones")], [r("BO1")], lambda q, T: [q.affine_select(T.BO1[:], T.ones[:], [[-16, 8], [0, 16]], O.is_ge, 0.0, 0, 1)])
     G(0.5, [r("BO1")], [r("BO")], lambda q, T: [q.affine_select(T.BO[:], T.BO1[:], [[16, 8], [0, 16]], O.is_ge, 0.0, 15, -1)])
     G(0.5, [r("ones")], [r("IB")], lambda q, T: [q.affine_select(T.IB[:], T.ones[:], [[-1, 128]], O.is_equal, 0.0, 0, 1)])
@@ -153,14 +155,14 @@ def build():
     V(v1(2048), [], [r("ZS")], fill("ZS", 0.0))
     V(v1(512), [], [r("R01")], fill("R01", 1.0))
     V(v1(64), [r("R01")], [r("R01")], fill(("R01", 0, 1024, 16), 0.0))
-    V(vh(2048), [r("sel")], [r("sel256")], ts("sel256", "sel", 256.0, O.mult))
+    V(vh(2048), [r("sel")], [r("sel128")], ts("sel128", "sel", 128.0, O.mult))
     V(tiny, [r("icol"), r("v2i")], [r("VW")], ts("VW", "v2i", "icol", O.add))
     V(tiny, [r("BO")], [r("blk32")], ts("blk32", ("BO", 0, 128, 16), 32.0, O.mult))
     V(tiny, [r("BO")], [r("blkn")], ts("blkn", ("BO", 0, 128, 16), -16.0, O.mult))
     V(v1(64), [], [r("RK")], fill("RK", 0.0))
-    V(tiny, [r("RK")], [r("RK")], fill(("RK", 0, 128, 16), 1048576.0))
+    V(tiny, [r("RK")], [r("RK")], fill(("RK", 0, 128, 16), 8388608.0))
     for c in range(2):
-        V(v1(128), [], [r("KS%d" % c)], fill("KS%d" % c, 0.0))
+        V(tiny, [], [r("KM%d" % c, 128, 144)], fill(("KM%d" % c, 128, 144), 8388608.0))
     V(vh(128), [r("IB"), r("ige1")], [r("pIm")], ts("pIm", "IB", "ige1", O.mult))
     V(vh(128), [r("pIm")], [r("nIm")], ts("nIm", "pIm", -1.0, O.mult))
     V(v1(128), [r("sel")], [r("Sel0")], copy("Sel0", ("sel", 0, 128)))
@@ -186,8 +188,10 @@ def build():
             a1 = a0 + n
             V(v1(n), [r(LU, a0, a1)], [r("L32", a0, a1)], copy(("L32", a0, a1), (LU, a0, a1)), "L32 c%d t%d" % (c, t))
             S(v1(n), [r("L32", a0, a1), r("k4")], [r("LQ", a0, a1)], act(("LQ", a0, a1), ("L32", a0, a1), AF.Identity, bias="k4"), "LQ c%d t%d" % (c, t))
-        dma("y", 2.0, [r("L32")], [r("DL")], "dl", lambda q, T: [q.dma_start(T.DL[:], T.L32[:])])
-        dma("y", P["wdma"], [r("DL")], [r("W")], "w", lambda q, T: [q.dma_start(T.W[j::16, 256 * j:4096], T.DL[:, 1:17 - j, :]) for j in range(1, 16)], 15)
+            dl = "DL%d" % c
+            dma("y", 2.2, [r("L32", a0, a1)], [r(dl)], "dl%d" % c, lambda q, T, dl=dl, a0=a0, a1=a1: [q.dma_start(T[dl][:], T.L32[:, a0:a1])])
+            dma("y", P["wdma"], [r(dl)], [r("W", 16 * a0, 16 * a1)], "w%d" % c,
+                lambda q, T, dl=dl, a0=a0, a1=a1, n=n: [q.dma_start(T.W[j::16, 16 * a0 + n * j:16 * a1], T[dl][:, 1:17 - j, :]) for j in range(1, 16)], 15)
         for c, (a0, n, pcs) in enumerate(CHUNKS):
             c0, b0 = 16 * a0, "pb%d0" % (c % 2)
             for p, (p0, pn) in enumerate(pcs):
@@ -212,18 +216,17 @@ def build():
                 cn = (b0, UNIT * k, UNIT * (k + 1))
                 PE(64 * 16, [r("H", lo, hi), r("sel")], [r(*cn)], mm(cn, [(nsel[j], ("H", lo + j, hi, 16)) for j in range(16)]), 16, "cnt" + ut)
                 V(v1(UNIT), [r(*cn), r(th)], [r("pas", u0, u1)], ts(("pas", u0, u1), cn, th, O.is_ge), "pass" + ut)
-        nwt = ("pb11", 256, 272)
-        PE(64 * 17, [r("pas"), r("sel256"), r("IB"), r("VW")], [r(*nwt)],
-           mm(nwt, [("IB", "VW")] + [(("sel256", 128 * k, 128 * k + 128), ("pas", k, 256, 16)) for k in range(16)]), 17, "nw t%d" % t)
+        nwt = ("pk1", 384, 400)
+        PE(64 * 17, [r("pas"), r("sel128"), r("IB"), r("VW")], [r(*nwt)],
+           mm(nwt, [("IB", "VW")] + [(("sel128", 128 * k, 128 * k + 128), ("pas", k, 256, 16)) for k in range(16)]), 17, "nw t%d" % t)
         V(tiny, [r(*nwt)], [r("OW")], copy("OW", nwt), "OW t%d" % t)
-        V(vg(256), [r("W"), r("OW"), r("pas")], [r("R1")], gtt("R1", ("W", 0, 4096), "OW", "pas", O.mult), "R1 t%d" % t)
         for k in range(2):
             npk = ("pk0", 256 + 128 * k, 384 + 128 * k)
             PE(256, [r("pas"), r("pIm"), r("nIm"), r("ones")], [r(*npk)], mm(npk, [("pIm", "ones"), ("nIm", ("pas", 128 * k, 128 * k + 128))]), 2, "np t%d" % t)
         for c, (a0, n, pcs) in enumerate(CHUNKS):
             a1, c0, c1, h0, h1 = a0 + n, 16 * a0, 16 * (a0 + n), a0 // 16, (a0 + n) // 16
             b = c % 2
-            b0, b1, b2, pk = "pb%d0" % b, "pb%d1" % b, "pb%d2" % b, "pk%d" % b
+            b0, b1, pk = "pb%d0" % b, "pb%d1" % b, "pk%d" % b
             tag = " c%d t%d" % (c, t)
             R = lambda x, a0=a0, a1=a1: r(x, a0, a1)
             Q = lambda x, a0=a0, a1=a1: (x, a0, a1)
@@ -237,7 +240,7 @@ def build():
             zs = ("ZS", c0, c1, 16)
             either("Z c%d" % c, vg(n), sg(n), [W("M"), r("OM", h0, h1)], [W("ZS")],
                    gcopy(True, zs, ("M", c0, c1), ("OM", h0, h1)), gcopy(False, zs, ("M", c0, c1), ("OM", h0, h1)), "Z" + tag)
-            s_, u_, q_ = (b0, 256, 256 + n), (b1, 0, n), (b2, 0, n)
+            s_, u_, q_ = (b0, 256, 256 + n), (b1, 0, n), (b1, 256, 256 + n)
             PE(2 * n, [R("XL"), r("WB"), r("ones"), r("c64")], [r(*s_)],
                lambda q, T, s_=s_, n=n, x=Q("XL"): [q.matmul(ap(s_)(T), T.ones[0:64, :], T.c64[:, 0:n], True, False), q.matmul(ap(s_)(T), T.WB[:], ap(x)(T), False, True)], 2, "s" + tag)
             V(v1(n), [r(*s_)], [R("B4")], ts(Q("B4"), s_, C35, O.add, -C35, O.add), "B4" + tag)
@@ -255,6 +258,10 @@ def build():
                 key = "c%d s%d" % (c, p)
                 pt = " %s t%d" % (key, t)
                 D, A, z16, d16, sv = ("D", lo, hi), ("A", lo, hi), ("ZS", lo, hi, 16), ("D", lo, hi, 16), ("sv", u0, u1)
+                if not last:
+                    f = 2.0 if side("C " + key) == "v" else 1.0
+                    either("Z2 " + key, v1(pn), v1(pn), [r("ZS", lo, hi)], [r("Z2", u0, u1)],
+                           ts(("Z2", u0, u1), z16, f, O.mult, -0.5, O.add), act(("Z2", u0, u1), z16, AF.Copy, bias=-0.5, scale=f), "Z2" + pt)
                 V(vh(m), [r("ZS", lo, hi), r("R01")], [r("Zx", lo, hi)], scan(("Zx", lo, hi), ("R01", 0, m), ("ZS", lo, hi), O.mult, O.add), "Zx" + pt)
                 modes.append(side("C " + key))
                 if modes[-1] == "v":
@@ -266,27 +273,23 @@ def build():
                     V(v1(2 * pn), [r(*D), r("ZS", lo, hi), r(*sv)], [r(*D)], tt(d16, sv, z16, O.max), "fx" + pt)
                     V(vh(m), [r(*D), r("Zx", lo, hi)], [r(*A)], scan(A, ("Zx", lo, hi), D, O.min, O.max), "A" + pt)
                     S(v1(pn), [r(*sv), r(*A)], [r(*D)], act(d16, sv, AF.Copy), "rs" + pt)
-                if not last:
-                    f = 2.0 if modes[-1] == "v" else 1.0
-                    either("Z2 " + key, v1(pn), v1(pn), [r("ZS", lo, hi)], [r("Z2", u0, u1)],
-                           ts(("Z2", u0, u1), z16, f, O.mult, -0.5, O.add), act(("Z2", u0, u1), z16, AF.Copy, bias=-0.5, scale=f), "Z2" + pt)
 
             def keyhalf(first, x, y, c0=c0, c1=c1, n=n, pk=pk):
                 def f(q, T):
-                    o = [q.matmul(T[pk][0:n, 0:128], T.ones[0:1, 0:n], T.irow[:], True, False)] if first else []
+                    o = [q.matmul(T[pk][0:n, 0:128], T.ones[0:1, 0:n], T.irow[:], True, False),
+                         q.matmul(T[pk][0:n, 0:128], T.ones[0:1, 0:n], T.grow[:], False, False)] if first else []
                     return o + [q.matmul(T[pk][0:n, i:128:16], T[x][:, c0 + i:c1:16], T[y][:], False, not first and i == 15) for i in range(16)]
                 return f
             hs = [("D", "blkn"), ("A", "blk32")]
             if "s" in modes:
                 hs.reverse()
             for k, (x, y) in enumerate(hs):
-                PE(64 * 16 + 128 * (1 - k), [W(x), r(y), r("irow"), r("ones")] + [r(pk, 0, 128)] * k, [r(pk, 0, 128)], keyhalf(k == 0, x, y), 17 - k, "key%d" % k + tag)
-            KM, KS, KB, OH = "KM%d" % b, "KS%d" % b, "KB%d" % b, "OH%d" % b
+                PE(64 * 16 + 256 * (1 - k), [W(x), r(y), r("irow"), r("grow"), r("ones")] + [r(pk, 0, 128)] * k, [r(pk, 0, 128)], keyhalf(k == 0, x, y), 18 - 2 * k, "key%d" % k + tag)
+            KM, KB, OH = "KM%d" % b, "KB%d" % b, "OH%d" % b
 
             def rows(x, lo=0, hi=128, st=1, n=n): return lambda T: T[x][0:n, lo:hi:st] if st > 1 else T[x][0:n, lo:hi]
-            V(v1(128), [r(pk, 0, 128), r("RK")], [r(KM)], lambda q, T, n=n, KM=KM, pk=pk: [q.tensor_tensor_scan(T[KM][0:n, :], T.RK[0:n, :], T[pk][0:n, 0:128], 0.0, O.max, O.min)], "KM" + tag)
-            V(tiny, [r(KM)], [r(KS)], lambda q, T, n=n, KM=KM, KS=KS: [q.tensor_copy(T[KS][0:n, ::16], T[KM][0:n, 15::16])], "KS" + tag)
-            V(v1(128), [r(KS), r("R01")], [r(KB)], lambda q, T, n=n, KS=KS, KB=KB: [q.tensor_tensor_scan(T[KB][0:n, :], T.R01[0:n, 0:128], T[KS][0:n, :], 0.0, O.mult, O.add)], "KB" + tag)
+            V(v1(128), [r(pk, 0, 128), r("RK")], [r(KM, 0, 128)], lambda q, T, n=n, KM=KM, pk=pk: [q.tensor_tensor_scan(T[KM][0:n, 0:128], T.RK[0:n, :], T[pk][0:n, 0:128], 0.0, O.max, O.min)], "KM" + tag)
+            V(v1(128), [r(KM), r("RK")], [r(KB)], lambda q, T, n=n, KM=KM, KB=KB: [q.tensor_tensor_scan(T[KB][0:n, :], T.RK[0:n, :], T[KM][0:n, 15:143], 0.0, O.max, O.min)], "KB" + tag)
             V(v1(128), [r(pk, 0, 128), r(KB)], [r(OH)], lambda q, T, n=n, KB=KB, pk=pk, OH=OH: [q.tensor_tensor(T[OH][0:n, :], T[pk][0:n, 0:128], T[KB][0:n, :], O.is_equal)], "OH" + tag)
             oh = (b0, 384, 384 + n)
             PE(n, [r(OH), r("IB")], [r(*oh)], lambda q, T, n=n, OH=OH, oh=oh: [q.matmul(ap(oh)(T), T[OH][0:n, :], T.IB[0:n, 0:n], True, True)], 1, "OHA" + tag)
@@ -298,10 +301,13 @@ def build():
                 V(tiny, [r(*tot)], [r("OT", h0, h1)], copy(("OT", h0, h1), tot), "OT" + tag)
                 V(vg(n), [W("D"), r("OT", h0, h1), R("Z2")], [R("tt")], gtt(Q("tt"), ("D", c0, c1), ("OT", h0, h1), Q("Z2"), O.add), "tt" + tag)
                 V(v1(n), [R("tt")], [R("Y2")], ts(Q("Y2"), Q("tt"), C24, O.add, -C24, O.add), "Y2" + tag)
-            np_, nl_ = ("pk0", 256 + a0, 256 + a1), (b2, 256, 256 + n)
+            np_, nl_ = ("pk0", 256 + a0, 256 + a1), ("pb%d2" % b, 0, n)
+            V(vg(n), [W("W"), r("OW", h0, h1), R("pas")], [R("R1")], gtt(Q("R1"), ("W", c0, c1), ("OW", h0, h1), Q("pas"), O.mult), "R1" + tag)
             V(v1(n), [r(*np_), R("cI")], [R("C1")], tt(Q("C1"), np_, Q("cI"), O.mult), "C1" + tag)
             V(v1(n), [r(*oh), R("cI")], [R("OC")], tt(Q("OC"), oh, Q("cI"), O.mult), "OC" + tag)
-            PE(12 * n, [R("R1"), R("C1"), R("OC"), r("IF"), r("Sel0")], [r(*nl_)], mm(nl_, [("IF", Q("R1")), ("IF", Q("C1")), ("Sel0", Q("OC"))]), 3, "nl" + tag)
+            PE(8 * n, [R("R1"), R("C1"), r("IF")], [r(*nl_)],
+               lambda q, T, x=Q("R1"), y=Q("C1"), o=nl_: [q.matmul(ap(o)(T), T.IF[:], ap(x)(T), True, False), q.matmul(ap(o)(T), T.IF[:], ap(y)(T), False, False)], 2, "nl0" + tag)
+            PE(4 * n, [R("OC"), r("Sel0"), r(*nl_)], [r(*nl_)], lambda q, T, x=Q("OC"), o=nl_: [q.matmul(ap(o)(T), T.Sel0[:], ap(x)(T), False, True)], 1, "nl1" + tag)
             if not last:
                 V(v1(n), [r(*nl_)], [R(NU)], copy(Q(NU), nl_), "NU" + tag)
                 add("g", 0.5, [R(NU)], [], ("send", t, c), "send" + tag, sem="sent")

@@ -12,7 +12,8 @@ for _n, _w, _d in (
         ("pI", 1, I32), ("iI", 1, I32), ("icol", 1, F32), ("i16", 1, F32), ("i32c", 1, F32),
         ("pthr", 1, F32), ("pthv", 1, F32), ("ige1", 1, F32), ("e15", 1, F32),
         ("ones", 128, BF), ("BO1", 128, BF), ("BO", 128, BF), ("IB", 128, BF), ("IF", 128, F32),
-        ("nI", 128, BF), ("n256I", 128, BF), ("pIm", 128, BF), ("nIm", 128, BF), ("WB", 128, BF), ("WB256", 128, BF),
+        ("pIm", 128, BF), ("nIm", 128, BF), ("BOd", 128, BF), ("OHm", 128, BF), ("BOf", 128, F32), ("BOf256", 128, F32),
+        ("UA", 256, F32), ("UO", 256, F32),
         ("S15", 128, BF), ("Sel0", 128, F32), ("LQ", 256, F32),
         ("sel", 2048, BF), ("isel", 2048, BF), ("wsel", 2048, BF), ("sel128", 2048, BF), ("blk32", 8, BF), ("blk16", 8, BF), ("blkn", 8, BF),
         ("v1i", 8, I32), ("v2i", 16, I32), ("v3i", 16, I32), ("VB", 8, BF), ("VW", 16, BF), ("SOp", 16, I32),
@@ -41,8 +42,8 @@ SEMAPHORES = ["cv", "cs", "ct", "cg", "sent", "ldt", "ldw", "ldk", "ldl", "ldx",
 P = {"cyc": 0.92e-3, "ga": 1.56, "pec": 0.5e-3, "wake": 0.18, "hop": 5.0, "wdma": 7.0}
 PLACE = {}
 PRI = {}
-SIDES = "ssvvvvssssssvssvvvvvssssvsvssssvvsvsssvvvs"
-RANKS = """-1053 350 636 58 307 -417 24 7 554 899 142 -285 -395 -437 -1677 -149 -409 -436 619 26 -740 333 -133 1078 405 2415 673 -982 -837 780 544 -708 -54 748 -40 -413 196 258 1 -876 -251 -104 -441 474 596 -22 613 800 -1231 215 -680 921 -14 411 660 -882 -439 50 -312 -84 38 146 -475 155 819 809 -182 -282 -30 467 314 338 789 105 -183 -60 1085 -31 -199 26 -394 -338 -98 -157 -236 -574 226 -543 -558 357 -75 -794 -247 250 -135 -377 -1804 69 -1492 -374 204 -943 506 -52 490 -134 484 108 576 -343 472 -216 153 535 -47 222 -1072 -619 -451 287 -607 -55 -304 210 259 -248 788 -831 -855 890 45 -490 229 -561 -601 155 741 295 -332 -60 -228 -596 -328 323 -344 60 -556 279 -181 -33 -271 -238 -385 -553 -508 357 -869 -66 -5 -410 932 374 520 502 202 -52 -1367 -146"""
+SIDES = "svssssssssvvvsvsvvssssssssvsvsssvvvvsvsvss"
+RANKS = """-1390 632 827 506 664 -870 -414 -646 440 822 -405 -395 632 -47 -2068 636 463 123 405 -1113 -586 100 256 947 447 2980 1247 -506 31 1199 231 -8 -277 803 223 -1047 -101 74 -971 -1330 -737 388 -75 716 327 513 1140 928 -1274 788 -1515 841 -727 402 1381 91 -1261 211 292 -469 -306 1419 -9 201 452 134 -287 -751 -781 1073 487 -452 33 -412 -1111 -1018 446 375 69 -641 1299 -481 173 307 -788 -491 -449 -727 -588 -1520 611 -1265 191 245 171 -939 -359 1543 248 -402 -2744 -408 -2445 -364 -490 -1360 922 -269 -517 -407 1066 108 1707 -343 290 430 -538 1058 635 549 -1249 -767 -333 255 -632 493 -561 -206 -691 652 255 36 914 -1112 -605 549 265 -381 908 -512 -601 599 741 -279 595 -581 728 -170 -897 -717 7 1542 -457 -745 804 -4 288 1004 -108 -55 -385 -319 -508 951 -592 252 -161 -519 1418 1071 1230 244 46 -1237 2 -204"""
 
 
 def side(key):
@@ -141,17 +142,17 @@ def build():
         V(tiny, [r("BO")], [r("sel")], copy(("sel", 16 * gg, 16 * gg + 129 * 15 + 1, 129), ("BO", 16 * gg, 16 * gg + 16)))
     V(tiny, [r("icol")], [r("i16")], ts("i16", "icol", 16.0, O.mult))
     V(tiny, [r("i16"), r("v1i")], [r("VB")], ts("VB", "v1i", "i16", O.add))
-    V(vh(128), [r("BO"), r("wc")], [r("WB")], ts("WB", "BO", "wc", O.mult))
-    V(vh(128), [r("WB")], [r("WB256")], ts("WB256", "WB", 256.0, O.mult))
+    V(v1(128), [r("BO")], [r("BOf")], copy("BOf", "BO"))
+    V(v1(128), [r("BO")], [r("BOf256")], ts("BOf256", "BO", 256.0, O.mult))
+    G(0.5, [r("BO")], [r("BOd")], lambda q, T: [q.affine_select(T.BOd[:], T.BO[:], [[-1, 128]], O.is_equal, 0.0, -1, 1)])
+    V(v1(256), [r("IB"), r("BOd")], [r("OHm")], tt("OHm", "IB", "BOd", O.subtract))
     V(tiny, [], [r("c64", 0, 1)], lambda q, T: [q.memset(T.c64[0:32, :], -64.0)])
     V(tiny, [], [r("c64", 1, 2)], lambda q, T: [q.memset(T.c64[32:64, :], 1.0 / 64)])
-    V(vh(128), [r("IB")], [r("nI")], ts("nI", "IB", -1.0, O.mult))
-    V(vh(128), [r("IB")], [r("n256I")], ts("n256I", "IB", -256.0, O.mult))
     V(v1(128), [r("IB")], [r("IF")], copy("IF", "IB"))
     V(tiny, [r("kc")], [r("k2")], ts("k2", "kc", -256.0, O.add))
-    V(tiny, [r("k2")], [r("sqb")], ts("sqb", "k2", 2.0, O.mult))
+    V(tiny, [r("k2")], [r("sqb")], ts("sqb", "k2", 2.0, O.mult, 511.875, O.add))
     V(tiny, [r("k2")], [r("k3")], ts("k3", "k2", "k2", O.mult, -4.0, O.mult))
-    V(tiny, [r("k3")], [r("k4")], ts("k4", "k3", -0.25, O.add))
+    V(tiny, [r("k3")], [r("k4")], ts("k4", "k3", -128.25, O.add))
     V(v1(2048), [], [r("ZS")], fill("ZS", 0.0))
     V(v1(512), [], [r("R01")], fill("R01", 1.0))
     V(v1(64), [r("R01")], [r("R01")], fill(("R01", 0, 1024, 16), 0.0))
@@ -213,9 +214,16 @@ def build():
                 else:
                     V(vh(m), [r("M", lo, hi), r("thv", t, t + 1)], [r("H", lo, hi)], ts(("H", lo, hi), ("M", lo, hi), ("thv", t, t + 1), O.is_ge), "I" + ut)
                     th = "pthv"
+                sa = (b0, 256 + UNIT * k, 256 + UNIT * (k + 1))
+                PE(64 * 17, [r("G", lo, hi), r("wsel"), r("ones"), r("c64")], [r(*sa)],
+                   lambda q, T, sa=sa, lo=lo, hi=hi: [q.matmul(ap(sa)(T), T.ones[0:64, :], T.c64[:, 0:UNIT], True, False)] +
+                   [q.matmul(ap(sa)(T), T.wsel[:, 128 * j:128 * j + 128], T.G[:, lo + j:hi:16], False, j == 15) for j in range(16)], 17, "sa" + ut)
                 cn = (b0, UNIT * k, UNIT * (k + 1))
                 PE(64 * 16, [r("H", lo, hi), r("sel")], [r(*cn)], mm(cn, [(nsel[j], ("H", lo + j, hi, 16)) for j in range(16)]), 16, "cnt" + ut)
                 V(v1(UNIT), [r(*cn), r(th)], [r("pas", u0, u1)], ts(("pas", u0, u1), cn, th, O.is_ge), "pass" + ut)
+            sa, ca, cb = (b0, 256, 256 + n), a0, a0 + n
+            V(v1(n), [r(*sa)], [r("B4", ca, cb)], ts(("B4", ca, cb), sa, C35, O.add, -C35, O.add), "B4 c%d t%d" % (c, t))
+            V(v1(n), [r(*sa), r("B4", ca, cb)], [r("UA", ca, cb)], tt(("UA", ca, cb), sa, ("B4", ca, cb), O.subtract), "UA c%d t%d" % (c, t))
         nwt = ("pk1", 384, 400)
         PE(64 * 17, [r("pas"), r("sel128"), r("IB"), r("VW")], [r(*nwt)],
            mm(nwt, [("IB", "VW")] + [(("sel128", 128 * k, 128 * k + 128), ("pas", k, 256, 16)) for k in range(16)]), 17, "nw t%d" % t)
@@ -235,23 +243,22 @@ def build():
             PE(64 * 17, [R("pas"), r("sel"), r("IB"), r("VB")], [r(*nbt)],
                mm(nbt, [("IB", ("VB", 0, n // 16))] + [(nsel[k], ("pas", a0 + k, a1, 16)) for k in range(16)]), 17, "nb" + tag)
             V(tiny, [r(*nbt)], [r("OM", h0, h1)], ts(("OM", h0, h1), nbt, -1.0, O.add), "OM" + tag)
-            either("XL c%d" % c, vg(n), sg(n), [W("G"), r("OM", h0, h1)], [R("XL")],
-                   gcopy(True, Q("XL"), ("G", c0, c1), ("OM", h0, h1)), gcopy(False, Q("XL"), ("G", c0, c1), ("OM", h0, h1)), "XL" + tag)
+            if not last:
+                either("XL c%d" % c, vg(n), sg(n), [W("G"), r("OM", h0, h1)], [R("XL")],
+                       gcopy(True, Q("XL"), ("G", c0, c1), ("OM", h0, h1)), gcopy(False, Q("XL"), ("G", c0, c1), ("OM", h0, h1)), "XL" + tag)
             zs = ("ZS", c0, c1, 16)
             either("Z c%d" % c, vg(n), sg(n), [W("M"), r("OM", h0, h1)], [W("ZS")],
                    gcopy(True, zs, ("M", c0, c1), ("OM", h0, h1)), gcopy(False, zs, ("M", c0, c1), ("OM", h0, h1)), "Z" + tag)
-            s_, u_, q_ = (b0, 256, 256 + n), (b1, 0, n), (b1, 256, 256 + n)
-            PE(2 * n, [R("XL"), r("WB"), r("ones"), r("c64")], [r(*s_)],
-               lambda q, T, s_=s_, n=n, x=Q("XL"): [q.matmul(ap(s_)(T), T.ones[0:64, :], T.c64[:, 0:n], True, False), q.matmul(ap(s_)(T), T.WB[:], ap(x)(T), False, True)], 2, "s" + tag)
-            V(v1(n), [r(*s_)], [R("B4")], ts(Q("B4"), s_, C35, O.add, -C35, O.add), "B4" + tag)
-            PE(2 * n, [R("XL"), r("WB"), r("nI"), R("B4")], [r(*u_)], mm(u_, [("WB", Q("XL")), ("nI", Q("B4"))]), 2, "u" + tag)
+            f_, u_, q_ = (b1, 384, 384 + n), (b1, 0, n), (b1, 256, 256 + n)
+            PE(n, [R("pas"), r("OHm")], [r(*f_)], mm(f_, [("OHm", Q("pas"))]), 1, "oneh" + tag)
+            V(v1(n), [r(*f_), R("UA")], [R("UO")], tt(Q("UO"), f_, Q("UA"), O.mult), "UO" + tag)
+            PE(4 * n, [R("UO"), r("BOf")], [r(*u_)], mm(u_, [("BOf", Q("UO"))]), 1, "u" + tag)
             S(v1(n), [r(*u_), r("sqb")], [R("SQ")], act(Q("SQ"), u_, AF.Square, bias="sqb", scale=0.25), "SQ" + tag)
-            PE(6 * n, [R("XL"), r("WB256"), r("n256I"), R("B4"), r("IF"), R("LQ")], [r(*q_)],
-               mm(q_, [("WB256", Q("XL")), ("n256I", Q("B4")), ("IF", Q("LQ"))]), 3, "q" + tag)
+            PE(8 * n, [R("UO"), r("BOf256"), r("IF"), R("LQ")], [r(*q_)], mm(q_, [("IF", Q("LQ")), ("BOf256", Q("UO"))]), 2, "q" + tag)
             V(v1(n), [r(*q_), R("SQ")], [R("xI")], tt(Q("xI"), q_, Q("SQ"), O.add), "x" + tag)
             V(v1(n), [R("xI")], [R("cI")], ts(Q("cI"), Q("xI"), 8191, O.bitwise_and), "and" + tag)
             V(v1(n), [R("cI")], [R("CU")], copy(Q("CU"), Q("cI")), "CU" + tag)
-            modes = []
+            first = []
             for p, (p0, pn) in enumerate(pcs):
                 lo, hi, m = c0 + 16 * p0, c0 + 16 * (p0 + pn), 16 * pn
                 u0, u1 = a0 + p0, a0 + p0 + pn
@@ -263,28 +270,28 @@ def build():
                     either("Z2 " + key, v1(pn), v1(pn), [r("ZS", lo, hi)], [r("Z2", u0, u1)],
                            ts(("Z2", u0, u1), z16, f, O.mult, -0.5, O.add), act(("Z2", u0, u1), z16, AF.Copy, bias=-0.5, scale=f), "Z2" + pt)
                 V(vh(m), [r("ZS", lo, hi), r("R01")], [r("Zx", lo, hi)], scan(("Zx", lo, hi), ("R01", 0, m), ("ZS", lo, hi), O.mult, O.add), "Zx" + pt)
-                modes.append(side("C " + key))
-                if modes[-1] == "v":
-                    V(vg(m), [r("X"), r("CU", u0, u1), r("Zx", lo, hi)], [r(*D)], gtt(D, ("X", 0, 8192), ("CU", u0, u1), ("Zx", lo, hi), O.subtract), "D" + pt)
-                    either("A " + key, vh(m), v1(m), [r(*D)], [r(*A)], ts(A, D, 0.0, O.max), act(A, D, AF.Relu), "A" + pt)
+                D0 = r("D0", lo, hi)
+                if side("C " + key) == "v":
+                    V(vg(m), [r("X"), r("CU", u0, u1), r("Zx", lo, hi)], [r(*D), D0], gtt(D, ("X", 0, 8192), ("CU", u0, u1), ("Zx", lo, hi), O.subtract), "D" + pt)
+                    first.append((p0, pn, d16, D0))
+                    either("A " + key, vh(m), v1(m), [r(*D), D0], [r(*A)], ts(A, D, 0.0, O.max), act(A, D, AF.Relu), "A" + pt)
                 else:
-                    S(sg(m), [r("X"), r("CU", u0, u1)], [r(*D)], gcopy(False, D, ("X", 0, 8192), ("CU", u0, u1)), "D" + pt)
-                    S(v1(pn), [r(*D)], [r(*sv)], act(sv, d16, AF.Copy), "sv" + pt)
-                    V(v1(2 * pn), [r(*D), r("ZS", lo, hi), r(*sv)], [r(*D)], tt(d16, sv, z16, O.max), "fx" + pt)
-                    V(vh(m), [r(*D), r("Zx", lo, hi)], [r(*A)], scan(A, ("Zx", lo, hi), D, O.min, O.max), "A" + pt)
-                    S(v1(pn), [r(*sv), r(*A)], [r(*D)], act(d16, sv, AF.Copy), "rs" + pt)
+                    S(sg(m), [r("X"), r("CU", u0, u1)], [r(*D), D0], gcopy(False, D, ("X", 0, 8192), ("CU", u0, u1)), "D" + pt)
+                    S(v1(pn), [D0], [r(*sv)], act(sv, d16, AF.Copy), "sv" + pt)
+                    first.append((p0, pn, sv, r(*sv)))
+                    V(v1(2 * pn), [r("ZS", lo, hi), r(*sv)], [D0], tt(d16, sv, z16, O.max), "fx" + pt)
+                    V(vh(m), [r(*D), D0, r("Zx", lo, hi)], [r(*A)], scan(A, ("Zx", lo, hi), D, O.min, O.max), "A" + pt)
+                    S(v1(pn), [r(*sv), r(*A)], [D0], act(d16, sv, AF.Copy), "rs" + pt)
 
-            def keyhalf(first, x, y, c0=c0, c1=c1, n=n, pk=pk):
-                def f(q, T):
-                    o = [q.matmul(T[pk][0:n, 0:128], T.ones[0:1, 0:n], T.irow[:], True, False),
-                         q.matmul(T[pk][0:n, 0:128], T.ones[0:1, 0:n], T.grow[:], False, False)] if first else []
-                    return o + [q.matmul(T[pk][0:n, i:128:16], T[x][:, c0 + i:c1:16], T[y][:], False, not first and i == 15) for i in range(16)]
-                return f
-            hs = [("D", "blkn"), ("A", "blk32")]
-            if "s" in modes:
-                hs.reverse()
-            for k, (x, y) in enumerate(hs):
-                PE(64 * 16 + 256 * (1 - k), [W(x), r(y), r("irow"), r("grow"), r("ones")] + [r(pk, 0, 128)] * k, [r(pk, 0, 128)], keyhalf(k == 0, x, y), 18 - 2 * k, "key%d" % k + tag)
+            def key0(q, T, c0=c0, c1=c1, n=n, pk=pk, first=first):
+                o = [q.matmul(T[pk][0:n, 0:128], T.ones[0:1, 0:n], T.irow[:], True, False), q.matmul(T[pk][0:n, 0:128], T.ones[0:1, 0:n], T.grow[:], False, False)]
+                o += [q.matmul(T[pk][0:n, i:128:16], T.D[:, c0 + i:c1:16], T.blkn[:], False, False) for i in range(1, 16)]
+                return o + [q.matmul(T[pk][p0:p0 + pn, 0:128:16], ap(x)(T), T.blkn[:], False, False) for (p0, pn, x, _) in first]
+
+            def key1(q, T, c0=c0, c1=c1, n=n, pk=pk):
+                return [q.matmul(T[pk][0:n, i:128:16], T.A[:, c0 + i:c1:16], T.blk32[:], False, i == 15) for i in range(16)]
+            PE(64 * 17 + 256, [W("D"), r("blkn"), r("irow"), r("grow"), r("ones")] + [f[3] for f in first], [r(pk, 0, 128)], key0, 17 + len(first), "key0" + tag)
+            PE(64 * 16, [W("A"), r("blk32"), r(pk, 0, 128)], [r(pk, 0, 128)], key1, 16, "key1" + tag)
             KM, KB, OH = "KM%d" % b, "KB%d" % b, "OH%d" % b
 
             def rows(x, lo=0, hi=128, st=1, n=n): return lambda T: T[x][0:n, lo:hi:st] if st > 1 else T[x][0:n, lo:hi]
@@ -299,7 +306,7 @@ def build():
                 PE(64 * 17, [R("OHA"), r("isel"), r("IB"), r("VB")], [r(*tot)],
                    mm(tot, [("IB", ("VB", 0, n // 16))] + [(("isel", 128 * k, 128 * k + 128), ("OHA", a0 + k, a1, 16)) for k in range(16)]), 17, "to" + tag)
                 V(tiny, [r(*tot)], [r("OT", h0, h1)], copy(("OT", h0, h1), tot), "OT" + tag)
-                V(vg(n), [W("D"), r("OT", h0, h1), R("Z2")], [R("tt")], gtt(Q("tt"), ("D", c0, c1), ("OT", h0, h1), Q("Z2"), O.add), "tt" + tag)
+                V(vg(n), [W("D"), W("D0"), r("OT", h0, h1), R("Z2")], [R("tt")], gtt(Q("tt"), ("D", c0, c1), ("OT", h0, h1), Q("Z2"), O.add), "tt" + tag)
                 V(v1(n), [R("tt")], [R("Y2")], ts(Q("Y2"), Q("tt"), C24, O.add, -C24, O.add), "Y2" + tag)
             np_, nl_ = ("pk0", 256 + a0, 256 + a1), ("pb%d2" % b, 0, n)
             V(vg(n), [W("W"), r("OW", h0, h1), R("pas")], [R("R1")], gtt(Q("R1"), ("W", c0, c1), ("OW", h0, h1), Q("pas"), O.mult), "R1" + tag)

from concourse.mybir import AluOpType, AxisListType, ActivationFunctionType

RO = 5
CHUNKS = [(0, 128, [(0, 32), (32, 32), (64, 32), (96, 32)]), (128, 128, [(0, 32), (32, 32), (64, 32), (96, 32)])]
UNIT = 64

BF, F32, I32, U16 = "bfloat16", "float32", "int32", "uint16"
SCRATCH = {"DL0": ("dram", [8, 16, 128], F32), "DL1": ("dram", [8, 16, 128], F32), "irow": ("sbuf", [1, 128], BF), "grow": ("sbuf", [1, 128], BF), "c64": ("sbuf", [64, 128], BF)}
for _n, _w, _d in (
        ("X", 8192, BF), ("TI", 256, I32), ("wi", 1, I32), ("ki", 1, I32), ("li", 8, I32),
        ("wc", 1, F32), ("kc", 1, F32), ("nl", 8, F32), ("lf", 8, F32), ("k2", 1, F32), ("k3", 1, F32), ("k4", 1, F32), ("sqb", 1, F32),
        ("pI", 1, I32), ("iI", 1, I32), ("icol", 1, F32), ("i16", 1, F32), ("i32c", 1, F32),
        ("pthr", 1, F32), ("pthv", 1, F32), ("ige1", 1, F32), ("e15", 1, F32),
        ("ones", 128, BF), ("BO1", 128, BF), ("BO", 128, BF), ("IB", 128, BF), ("IF", 128, F32),
        ("pIm", 128, BF), ("nIm", 128, BF), ("BOd", 128, BF), ("OHm", 128, BF), ("BOf", 128, F32), ("BOf256", 128, F32),
        ("UA", 256, F32), ("UO", 256, F32),
        ("S15", 128, BF), ("Sel0", 128, F32), ("LQ", 256, F32),
        ("sel", 2048, BF), ("isel", 2048, BF), ("wsel", 2048, BF), ("sel128", 2048, BF), ("blk32", 8, BF), ("blk16", 8, BF), ("blkn", 8, BF),
        ("v1i", 8, I32), ("v2i", 16, I32), ("v3i", 16, I32), ("VB", 8, BF), ("VW", 16, BF), ("SOp", 16, I32),
        ("R01", 1024, BF), ("RB", 1024, BF), ("RK", 128, BF), ("half", 128, BF), ("W", 4096, F32),
        ("soA", 16, I32), ("soB", 16, I32), ("soC", 16, I32), ("SO", 16, U16),
        ("er", 1, F32), ("eI", 1, I32), ("eJ", 1, I32), ("nth", 8, F32), ("thv", 8, F32),
        ("ZS", 4096, BF), ("G", 4096, BF), ("M", 4096, BF), ("H", 4096, BF), ("Zx", 4096, BF), ("D", 4096, BF), ("A", 4096, BF),
        ("pas", 256, BF), ("OM", 16, U16), ("OW", 16, U16), ("OT", 16, U16), ("XL", 256, BF), ("Z2", 256, F32), ("B4", 256, BF),
        ("SQ", 256, F32), ("xI", 256, I32), ("cI", 256, I32), ("CU", 256, U16), ("L32", 256, F32), ("OHA", 256, BF), ("sv", 256, BF),
        ("OC", 256, F32), ("C1", 256, F32), ("R1", 256, F32), ("tt", 256, F32), ("Y2", 256, BF), ("yls", 256, F32), ("yzs", 256, F32)):
    SCRATCH[_n] = ("sbuf", [128, _w], _d)
for _c in range(2):
    SCRATCH["KM%d" % _c] = ("sbuf", [128, 144], F32)
    SCRATCH["KB%d" % _c] = ("sbuf", [128, 128], F32)
    SCRATCH["OH%d" % _c] = ("sbuf", [128, 128], BF)
    for _b in ("pb%d0", "pb%d1", "pb%d2", "pk%d"):
        SCRATCH[_b % _c] = ("psum", [128, 512], F32)
for _t in range(RO):
    SCRATCH["LU%d" % _t] = ("sbuf", [128, 256], U16)
    if _t < RO - 1:
        SCRATCH["NU%d" % _t] = ("sbuf", [128, 256], U16)

SEMAPHORES = ["cv", "cs", "ct", "cg", "sent", "ldt", "ldw", "ldk", "ldl", "ldx", "ldy"] + \
    ["%s%d" % (a, c) for a in ("oz", "ol", "dl", "w") for c in range(len(CHUNKS))] + ["arr%d%d" % (t, c) for t in range(1, RO) for c in range(len(CHUNKS))]

P = {"cyc": 0.92e-3, "ga": 1.56, "pec": 0.5e-3, "wake": 0.18, "hop": 5.0, "wdma": 7.0}
PLACE = {}
PRI = {}
SIDES = "svssssssssvvvsvsvvssssssssvsvsssvvvvsvsvss"
RANKS = """-1390 632 827 506 664 -870 -414 -646 440 822 -405 -395 632 -47 -2068 636 463 123 405 -1113 -586 100 256 947 447 2980 1247 -506 31 1199 231 -8 -277 803 223 -1047 -101 74 -971 -1330 -737 388 -75 716 327 513 1140 928 -1274 788 -1515 841 -727 402 1381 91 -1261 211 292 -469 -306 1419 -9 201 452 134 -287 -751 -781 1073 487 -452 33 -412 -1111 -1018 446 375 69 -641 1299 -481 173 307 -788 -491 -449 -727 -588 -1520 611 -1265 191 245 171 -939 -359 1543 248 -402 -2744 -408 -2445 -364 -490 -1360 922 -269 -517 -407 1066 108 1707 -343 290 430 -538 1058 635 549 -1249 -767 -333 255 -632 493 -561 -206 -691 652 255 36 914 -1112 -605 549 265 -381 908 -512 -601 599 741 -279 595 -581 728 -170 -897 -717 7 1542 -457 -745 804 -4 288 1004 -108 -55 -385 -319 -508 951 -592 252 -161 -519 1418 1071 1230 244 46 -1237 2 -204"""


def side(key):
    return PLACE.get(key, "s")


def build():
    O, AF = AluOpType, ActivationFunctionType
    ops = []
    cyc, pec = P["cyc"], P["pec"]

    def v1(n): return max(64, n) * cyc
    def vh(n): return max(64, n / 2) * cyc
    def vg(n): return 0.055 + n * P["ga"] * cyc
    def sg(n): return 0.07 + n * P["ga"] * cyc
    tiny = v1(1)

    def add(eng, cost, reads, writes, fn, name="", sem=None, n=1):
        ops.append({"eng": eng, "cost": cost, "reads": reads, "writes": writes, "fn": fn, "name": name, "sem": sem, "n": n, "id": len(ops)})

    def V(cost, reads, writes, fn, name=""): add("v", cost, reads, writes, fn, name)
    def S(cost, reads, writes, fn, name=""): add("s", cost, reads, writes, fn, name)
    def PE(cyc_n, reads, writes, fn, n, name=""): add("t", cyc_n * pec, reads, writes, fn, name, n=n)
    def r(b, lo=0, hi=100000): return (b, lo, hi)

    def ap(a):
        if isinstance(a, (int, float)):
            return lambda T: a
        if isinstance(a, str):
            return lambda T: T[a][:]
        if len(a) == 3:
            return lambda T: T[a[0]][:, a[1]:a[2]]
        return lambda T: T[a[0]][:, a[1]:a[2]:a[3]]

    def copy(out, in_): return lambda q, T: [q.tensor_copy(ap(out)(T), ap(in_)(T))]
    def fill(out, x): return lambda q, T: [q.memset(ap(out)(T), x)]
    def tt(out, a, b, op): return lambda q, T: [q.tensor_tensor(ap(out)(T), ap(a)(T), ap(b)(T), op)]
    def scan(out, a, b, o0, o1): return lambda q, T: [q.tensor_tensor_scan(ap(out)(T), ap(a)(T), ap(b)(T), 0.0, o0, o1)]
    def act(out, in_, f, **kw): return lambda q, T: [q.activation(ap(out)(T), ap(in_)(T), f, **dict((k, ap(x)(T)) for k, x in kw.items()))]

    def ts(out, in0, s1, o1, s2=None, o2=None):
        if o2 is None:
            return lambda q, T: [q.tensor_scalar(ap(out)(T), ap(in0)(T), ap(s1)(T), None, o1)]
        return lambda q, T: [q.tensor_scalar(ap(out)(T), ap(in0)(T), ap(s1)(T), ap(s2)(T), o1, o2)]

    def gcopy(q_v, out, win, off):
        if q_v:
            return lambda q, T: [q.tensor_copy(ap(out)(T), ap(win)(T).indirect(ap(off)(T)))]
        return lambda q, T: [q.activation(ap(out)(T), ap(win)(T).indirect(ap(off)(T)), AF.Copy)]

    def gtt(out, win, off, b, op): return lambda q, T: [q.tensor_tensor(ap(out)(T), ap(win)(T).indirect(ap(off)(T)), ap(b)(T), op)]
    def mm(out, terms): return lambda q, T: [q.matmul(ap(out)(T), ap(a)(T), ap(b)(T), i == 0, i == len(terms) - 1) for i, (a, b) in enumerate(terms)]

    def either(key, nv, ns, reads, writes, fv, fs, name):
        if side(key) == "v":
            V(nv, reads, writes, fv, name)
        else:
            S(ns, reads, writes, fs, name)

    def dma(eng, cost, reads, writes, sem, fn, k=1): add(eng, cost, reads, writes, fn, sem, sem=sem, n=k)
    dma("y", 2.0, [], [r("TI")], "ldt", lambda q, T: [q.dma_start(T.TI[:], T.tube[:])])
    dma("y", 2.0, [], [r("wi")], "ldw", lambda q, T: [q.dma_start(T.wi[:], T.wt[:])])
    dma("y", 2.0, [], [r("ki")], "ldk", lambda q, T: [q.dma_start(T.ki[:], T.kn[:])])
    dma("y", 2.0, [], [r("li")], "ldl", lambda q, T: [q.dma_start(T.li[:, 0:5], T.lim[:])])
    dma("y", 9.0, [], [r("X", 0, 4096)], "ldx", lambda q, T: [q.dma_start(T.X[:, 0:4096], T.field[:, 0:4096])])
    dma("s", 9.0, [], [r("X", 4096, 8192)], "ldy", lambda q, T: [q.dma_start(T.X[:, 4096:8192], T.field[:, 4096:8192])])
    def G(cost, reads, writes, fn): add("g", cost, reads, writes, fn)
    V(v1(64), [], [r("ones")], fill("ones", 1.0))
    G(0.4, [], [r("pI")], lambda q, T: [q.iota(T.pI[:], [[0, 1]], 0, 1)])
    G(0.4, [], [r("v1i")], lambda q, T: [q.iota(T.v1i[:], [[256, 8]], 0, 0)])
    G(0.4, [], [r("v2i")], lambda q, T: [q.iota(T.v2i[:], [[0, 2], [16, 8]], -128, 0)])
    G(0.4, [], [r("v3i")], lambda q, T: [q.iota(T.v3i[:], [[512, 16]], 0, 0)])
    G(0.6, [], [r("irow")], lambda q, T: [q.iota(T.irow[:], [[0, 8], [1, 16]], 0, 0, allow_small_or_imprecise_dtypes=True)])
    G(0.6, [], [r("grow")], lambda q, T: [q.iota(T.grow[:], [[16384, 8], [0, 16]], 0, 0, allow_small_or_imprecise_dtypes=True)])
    V(tiny, [r("grow")], [r("grow")], lambda q, T: [q.tensor_scalar(T.grow[:], T.grow[:], 16.0, None, O.mult)])
    G(0.5, [r("ones")], [r("BO1")], lambda q, T: [q.affine_select(T.BO1[:], T.ones[:], [[-16, 8], [0, 16]], O.is_ge, 0.0, 0, 1)])
    G(0.5, [r("BO1")], [r("BO")], lambda q, T: [q.affine_select(T.BO[:], T.BO1[:], [[16, 8], [0, 16]], O.is_ge, 0.0, 15, -1)])
    G(0.5, [r("ones")], [r("IB")], lambda q, T: [q.affine_select(T.IB[:], T.ones[:], [[-1, 128]], O.is_equal, 0.0, 0, 1)])
    V(v1(256), [r("TI")], [r("LU0")], copy("LU0", "TI"))
    V(v1(1024), [], [r("RB")], fill("RB", 0.0))
    V(v1(64), [r("RB")], [r("RB")], fill(("RB", 0, 1024, 16), 256.0))
    V(tiny, [r("pI")], [r("iI")], ts("iI", "pI", 15, O.bitwise_and))
    V(tiny, [r("iI")], [r("icol")], copy("icol", "iI"))
    V(tiny, [r("wi")], [r("wc")], copy("wc", "wi"))
    V(tiny, [r("ki")], [r("kc")], copy("kc", "ki"))
    V(tiny, [r("li")], [r("lf")], copy(("lf", 0, 5), ("li", 0, 5)))
    V(tiny, [r("lf")], [r("nl")], ts(("nl", 0, 5), ("lf", 0, 5), -1.0, O.mult, 0.5, O.add))
    V(tiny, [r("nl")], [r("nth", 0, 1)], copy(("nth", 0, 1), ("nl", 0, 1)))
    V(tiny, [r("lf")], [r("thv", 0, 1)], copy(("thv", 0, 1), ("lf", 0, 1)))
    V(tiny, [r("icol")], [r("ige1")], ts("ige1", "icol", 1.0, O.is_ge))
    V(tiny, [r("icol")], [r("e15")], ts("e15", "icol", 15.0, O.is_equal))
    V(tiny, [r("ige1")], [r("pthr")], ts("pthr", "ige1", 102.0, O.mult, -101.0, O.add))
    V(tiny, [r("ige1")], [r("pthv")], ts("pthv", "ige1", 109.5, O.mult, -101.0, O.add))
    V(v1(1024), [], [r("sel")], fill("sel", 0.0))
    for gg in range(8):
        V(tiny, [r("BO")], [r("sel")], copy(("sel", 16 * gg, 16 * gg + 129 * 15 + 1, 129), ("BO", 16 * gg, 16 * gg + 16)))
    V(tiny, [r("icol")], [r("i16")], ts("i16", "icol", 16.0, O.mult))
    V(tiny, [r("i16"), r("v1i")], [r("VB")], ts("VB", "v1i", "i16", O.add))
    V(v1(128), [r("BO")], [r("BOf")], copy("BOf", "BO"))
    V(v1(128), [r("BO")], [r("BOf256")], ts("BOf256", "BO", 256.0, O.mult))
    G(0.5, [r("BO")], [r("BOd")], lambda q, T: [q.affine_select(T.BOd[:], T.BO[:], [[-1, 128]], O.is_equal, 0.0, -1, 1)])
    V(v1(256), [r("IB"), r("BOd")], [r("OHm")], tt("OHm", "IB", "BOd", O.subtract))
    V(tiny, [], [r("c64", 0, 1)], lambda q, T: [q.memset(T.c64[0:32, :], -64.0)])
    V(tiny, [], [r("c64", 1, 2)], lambda q, T: [q.memset(T.c64[32:64, :], 1.0 / 64)])
    V(v1(128), [r("IB")], [r("IF")], copy("IF", "IB"))
    V(tiny, [r("kc")], [r("k2")], ts("k2", "kc", -256.0, O.add))
    V(tiny, [r("k2")], [r("sqb")], ts("sqb", "k2", 2.0, O.mult, 511.875, O.add))
    V(tiny, [r("k2")], [r("k3")], ts("k3", "k2", "k2", O.mult, -4.0, O.mult))
    V(tiny, [r("k3")], [r("k4")], ts("k4", "k3", -128.25, O.add))
    V(v1(2048), [], [r("ZS")], fill("ZS", 0.0))
    V(v1(512), [], [r("R01")], fill("R01", 1.0))
    V(v1(64), [r("R01")], [r("R01")], fill(("R01", 0, 1024, 16), 0.0))
    V(vh(2048), [r("sel")], [r("sel128")], ts("sel128", "sel", 128.0, O.mult))
    V(tiny, [r("icol"), r("v2i")], [r("VW")], ts("VW", "v2i", "icol", O.add))
    V(tiny, [r("BO")], [r("blk32")], ts("blk32", ("BO", 0, 128, 16), 32.0, O.mult))
    V(tiny, [r("BO")], [r("blkn")], ts("blkn", ("BO", 0, 128, 16), -16.0, O.mult))
    V(v1(64), [], [r("RK")], fill("RK", 0.0))
    V(tiny, [r("RK")], [r("RK")], fill(("RK", 0, 128, 16), 8388608.0))
    for c in range(2):
        V(tiny, [], [r("KM%d" % c, 128, 144)], fill(("KM%d" % c, 128, 144), 8388608.0))
    V(vh(128), [r("IB"), r("ige1")], [r("pIm")], ts("pIm", "IB", "ige1", O.mult))
    V(vh(128), [r("pIm")], [r("nIm")], ts("nIm", "pIm", -1.0, O.mult))
    V(v1(128), [r("sel")], [r("Sel0")], copy("Sel0", ("sel", 0, 128)))
    V(vh(2048), [r("sel"), r("icol")], [r("isel")], ts("isel", "sel", "icol", O.mult))
    V(vh(2048), [r("sel"), r("wc")], [r("wsel")], ts("wsel", "sel", "wc", O.mult))
    V(tiny, [r("icol")], [r("i32c")], ts("i32c", "icol", 32.0, O.mult))
    V(tiny, [r("v3i"), r("i32c")], [r("SOp")], ts("SOp", "v3i", "i32c", O.add))
    V(v1(64), [], [r("half")], fill("half", 0.5))
    V(vh(128), [r("ones"), r("e15")], [r("S15")], ts("S15", "ones", "e15", O.mult))
    for c in range(2):
        S(v1(2048), [r("ZS")], [r("W", 2048 * c, 2048 * c + 2048)], act(("W", 2048 * c, 2048 * c + 2048), ("ZS", 2048 * c, 2048 * c + 2048), AF.Copy))

    C35 = 1.5 * 2.0 ** 35
    C24 = 1.5 * 2.0 ** 24
    nsel = [("sel", 128 * k, 128 * k + 128) for k in range(16)]
    for t in range(RO):
        last = t == RO - 1
        LU, NU = "LU%d" % t, "NU%d" % t
        if t:
            for c, (a0, n, pcs) in enumerate(CHUNKS):
                add("x", P["hop"], [r("NU%d" % (t - 1), a0, a0 + n)], [r(LU, a0, a0 + n)], None, "arr", sem="arr%d%d" % (t, c))
        for c, (a0, n, pcs) in enumerate(CHUNKS):
            a1 = a0 + n
            V(v1(n), [r(LU, a0, a1)], [r("L32", a0, a1)], copy(("L32", a0, a1), (LU, a0, a1)), "L32 c%d t%d" % (c, t))
            S(v1(n), [r("L32", a0, a1), r("k4")], [r("LQ", a0, a1)], act(("LQ", a0, a1), ("L32", a0, a1), AF.Identity, bias="k4"), "LQ c%d t%d" % (c, t))
            dl = "DL%d" % c
            dma("y", 2.2, [r("L32", a0, a1)], [r(dl)], "dl%d" % c, lambda q, T, dl=dl, a0=a0, a1=a1: [q.dma_start(T[dl][:], T.L32[:, a0:a1])])
            dma("y", P["wdma"], [r(dl)], [r("W", 16 * a0, 16 * a1)], "w%d" % c,
                lambda q, T, dl=dl, a0=a0, a1=a1, n=n: [q.dma_start(T.W[j::16, 16 * a0 + n * j:16 * a1], T[dl][:, 1:17 - j, :]) for j in range(1, 16)], 15)
        for c, (a0, n, pcs) in enumerate(CHUNKS):
            c0, b0 = 16 * a0, "pb%d0" % (c % 2)
            for p, (p0, pn) in enumerate(pcs):
                lo, hi, m = c0 + 16 * p0, c0 + 16 * (p0 + pn), 16 * pn
                u0, u1 = a0 + p0, a0 + p0 + pn
                key = "c%d s%d" % (c, p)
                pt = " %s t%d" % (key, t)
                either("G " + key, vg(m), sg(m), [r("X"), r(LU, u0, u1)], [r("G", lo, hi)],
                       gcopy(True, ("G", lo, hi), ("X", 0, 8192), (LU, u0, u1)), gcopy(False, ("G", lo, hi), ("X", 0, 8192), (LU, u0, u1)), "G" + pt)
                V(vh(m), [r("G", lo, hi), r("RB")], [r("M", lo, hi)], scan(("M", lo, hi), ("RB", 0, m), ("G", lo, hi), O.max, O.min), "M" + pt)
            for k in range(n // UNIT):
                lo, hi, m = c0 + 16 * UNIT * k, c0 + 16 * UNIT * (k + 1), 16 * UNIT
                u0, u1 = a0 + UNIT * k, a0 + UNIT * (k + 1)
                key = "c%d u%d" % (c, k)
                ut = " %s t%d" % (key, t)
                if side("I " + key) == "s":
                    S(v1(m), [r("M", lo, hi), r("nth", t, t + 1)], [r("H", lo, hi)], act(("H", lo, hi), ("M", lo, hi), AF.Sign, bias=("nth", t, t + 1)), "I" + ut)
                    th = "pthr"
                else:
                    V(vh(m), [r("M", lo, hi), r("thv", t, t + 1)], [r("H", lo, hi)], ts(("H", lo, hi), ("M", lo, hi), ("thv", t, t + 1), O.is_ge), "I" + ut)
                    th = "pthv"
                sa = (b0, 256 + UNIT * k, 256 + UNIT * (k + 1))
                PE(64 * 17, [r("G", lo, hi), r("wsel"), r("ones"), r("c64")], [r(*sa)],
                   lambda q, T, sa=sa, lo=lo, hi=hi: [q.matmul(ap(sa)(T), T.ones[0:64, :], T.c64[:, 0:UNIT], True, False)] +
                   [q.matmul(ap(sa)(T), T.wsel[:, 128 * j:128 * j + 128], T.G[:, lo + j:hi:16], False, j == 15) for j in range(16)], 17, "sa" + ut)
                cn = (b0, UNIT * k, UNIT * (k + 1))
                PE(64 * 16, [r("H", lo, hi), r("sel")], [r(*cn)], mm(cn, [(nsel[j], ("H", lo + j, hi, 16)) for j in range(16)]), 16, "cnt" + ut)
                V(v1(UNIT), [r(*cn), r(th)], [r("pas", u0, u1)], ts(("pas", u0, u1), cn, th, O.is_ge), "pass" + ut)
            sa, ca, cb = (b0, 256, 256 + n), a0, a0 + n
            V(v1(n), [r(*sa)], [r("B4", ca, cb)], ts(("B4", ca, cb), sa, C35, O.add, -C35, O.add), "B4 c%d t%d" % (c, t))
            V(v1(n), [r(*sa), r("B4", ca, cb)], [r("UA", ca, cb)], tt(("UA", ca, cb), sa, ("B4", ca, cb), O.subtract), "UA c%d t%d" % (c, t))
        nwt = ("pk1", 384, 400)
        PE(64 * 17, [r("pas"), r("sel128"), r("IB"), r("VW")], [r(*nwt)],
           mm(nwt, [("IB", "VW")] + [(("sel128", 128 * k, 128 * k + 128), ("pas", k, 256, 16)) for k in range(16)]), 17, "nw t%d" % t)
        V(tiny, [r(*nwt)], [r("OW")], copy("OW", nwt), "OW t%d" % t)
        for k in range(2):
            npk = ("pk0", 256 + 128 * k, 384 + 128 * k)
            PE(256, [r("pas"), r("pIm"), r("nIm"), r("ones")], [r(*npk)], mm(npk, [("pIm", "ones"), ("nIm", ("pas", 128 * k, 128 * k + 128))]), 2, "np t%d" % t)
        for c, (a0, n, pcs) in enumerate(CHUNKS):
            a1, c0, c1, h0, h1 = a0 + n, 16 * a0, 16 * (a0 + n), a0 // 16, (a0 + n) // 16
            b = c % 2
            b0, b1, pk = "pb%d0" % b, "pb%d1" % b, "pk%d" % b
            tag = " c%d t%d" % (c, t)
            R = lambda x, a0=a0, a1=a1: r(x, a0, a1)
            Q = lambda x, a0=a0, a1=a1: (x, a0, a1)
            W = lambda x, c0=c0, c1=c1: r(x, c0, c1)
            nbt = (b0, 128, 128 + n // 16)
            PE(64 * 17, [R("pas"), r("sel"), r("IB"), r("VB")], [r(*nbt)],
               mm(nbt, [("IB", ("VB", 0, n // 16))] + [(nsel[k], ("pas", a0 + k, a1, 16)) for k in range(16)]), 17, "nb" + tag)
            V(tiny, [r(*nbt)], [r("OM", h0, h1)], ts(("OM", h0, h1), nbt, -1.0, O.add), "OM" + tag)
            if not last:
                either("XL c%d" % c, vg(n), sg(n), [W("G"), r("OM", h0, h1)], [R("XL")],
                       gcopy(True, Q("XL"), ("G", c0, c1), ("OM", h0, h1)), gcopy(False, Q("XL"), ("G", c0, c1), ("OM", h0, h1)), "XL" + tag)
            zs = ("ZS", c0, c1, 16)
            either("Z c%d" % c, vg(n), sg(n), [W("M"), r("OM", h0, h1)], [W("ZS")],
                   gcopy(True, zs, ("M", c0, c1), ("OM", h0, h1)), gcopy(False, zs, ("M", c0, c1), ("OM", h0, h1)), "Z" + tag)
            f_, u_, q_ = (b1, 384, 384 + n), (b1, 0, n), (b1, 256, 256 + n)
            PE(n, [R("pas"), r("OHm")], [r(*f_)], mm(f_, [("OHm", Q("pas"))]), 1, "oneh" + tag)
            V(v1(n), [r(*f_), R("UA")], [R("UO")], tt(Q("UO"), f_, Q("UA"), O.mult), "UO" + tag)
            PE(4 * n, [R("UO"), r("BOf")], [r(*u_)], mm(u_, [("BOf", Q("UO"))]), 1, "u" + tag)
            S(v1(n), [r(*u_), r("sqb")], [R("SQ")], act(Q("SQ"), u_, AF.Square, bias="sqb", scale=0.25), "SQ" + tag)
            PE(8 * n, [R("UO"), r("BOf256"), r("IF"), R("LQ")], [r(*q_)], mm(q_, [("IF", Q("LQ")), ("BOf256", Q("UO"))]), 2, "q" + tag)
            V(v1(n), [r(*q_), R("SQ")], [R("xI")], tt(Q("xI"), q_, Q("SQ"), O.add), "x" + tag)
            V(v1(n), [R("xI")], [R("cI")], ts(Q("cI"), Q("xI"), 8191, O.bitwise_and), "and" + tag)
            V(v1(n), [R("cI")], [R("CU")], copy(Q("CU"), Q("cI")), "CU" + tag)
            first = []
            for p, (p0, pn) in enumerate(pcs):
                lo, hi, m = c0 + 16 * p0, c0 + 16 * (p0 + pn), 16 * pn
                u0, u1 = a0 + p0, a0 + p0 + pn
                key = "c%d s%d" % (c, p)
                pt = " %s t%d" % (key, t)
                D, A, z16, d16, sv = ("D", lo, hi), ("A", lo, hi), ("ZS", lo, hi, 16), ("D", lo, hi, 16), ("sv", u0, u1)
                if not last:
                    f = 2.0 if side("C " + key) == "v" else 1.0
                    either("Z2 " + key, v1(pn), v1(pn), [r("ZS", lo, hi)], [r("Z2", u0, u1)],
                           ts(("Z2", u0, u1), z16, f, O.mult, -0.5, O.add), act(("Z2", u0, u1), z16, AF.Copy, bias=-0.5, scale=f), "Z2" + pt)
                V(vh(m), [r("ZS", lo, hi), r("R01")], [r("Zx", lo, hi)], scan(("Zx", lo, hi), ("R01", 0, m), ("ZS", lo, hi), O.mult, O.add), "Zx" + pt)
                D0 = r("D0", lo, hi)
                if side("C " + key) == "v":
                    V(vg(m), [r("X"), r("CU", u0, u1), r("Zx", lo, hi)], [r(*D), D0], gtt(D, ("X", 0, 8192), ("CU", u0, u1), ("Zx", lo, hi), O.subtract), "D" + pt)
                    first.append((p0, pn, d16, D0))
                    either("A " + key, vh(m), v1(m), [r(*D), D0], [r(*A)], ts(A, D, 0.0, O.max), act(A, D, AF.Relu), "A" + pt)
                else:
                    S(sg(m), [r("X"), r("CU", u0, u1)], [r(*D), D0], gcopy(False, D, ("X", 0, 8192), ("CU", u0, u1)), "D" + pt)
                    S(v1(pn), [D0], [r(*sv)], act(sv, d16, AF.Copy), "sv" + pt)
                    first.append((p0, pn, sv, r(*sv)))
                    V(v1(2 * pn), [r("ZS", lo, hi), r(*sv)], [D0], tt(d16, sv, z16, O.max), "fx" + pt)
                    V(vh(m), [r(*D), D0, r("Zx", lo, hi)], [r(*A)], scan(A, ("Zx", lo, hi), D, O.min, O.max), "A" + pt)
                    S(v1(pn), [r(*sv), r(*A)], [D0], act(d16, sv, AF.Copy), "rs" + pt)

            def key0(q, T, c0=c0, c1=c1, n=n, pk=pk, first=first):
                o = [q.matmul(T[pk][0:n, 0:128], T.ones[0:1, 0:n], T.irow[:], True, False), q.matmul(T[pk][0:n, 0:128], T.ones[0:1, 0:n], T.grow[:], False, False)]
                o += [q.matmul(T[pk][0:n, i:128:16], T.D[:, c0 + i:c1:16], T.blkn[:], False, False) for i in range(1, 16)]
                return o + [q.matmul(T[pk][p0:p0 + pn, 0:128:16], ap(x)(T), T.blkn[:], False, False) for (p0, pn, x, _) in first]

            def key1(q, T, c0=c0, c1=c1, n=n, pk=pk):
                return [q.matmul(T[pk][0:n, i:128:16], T.A[:, c0 + i:c1:16], T.blk32[:], False, i == 15) for i in range(16)]
            PE(64 * 17 + 256, [W("D"), r("blkn"), r("irow"), r("grow"), r("ones")] + [f[3] for f in first], [r(pk, 0, 128)], key0, 17 + len(first), "key0" + tag)
            PE(64 * 16, [W("A"), r("blk32"), r(pk, 0, 128)], [r(pk, 0, 128)], key1, 16, "key1" + tag)
            KM, KB, OH = "KM%d" % b, "KB%d" % b, "OH%d" % b

            def rows(x, lo=0, hi=128, st=1, n=n): return lambda T: T[x][0:n, lo:hi:st] if st > 1 else T[x][0:n, lo:hi]
            V(v1(128), [r(pk, 0, 128), r("RK")], [r(KM, 0, 128)], lambda q, T, n=n, KM=KM, pk=pk: [q.tensor_tensor_scan(T[KM][0:n, 0:128], T.RK[0:n, :], T[pk][0:n, 0:128], 0.0, O.max, O.min)], "KM" + tag)
            V(v1(128), [r(KM), r("RK")], [r(KB)], lambda q, T, n=n, KM=KM, KB=KB: [q.tensor_tensor_scan(T[KB][0:n, :], T.RK[0:n, :], T[KM][0:n, 15:143], 0.0, O.max, O.min)], "KB" + tag)
            V(v1(128), [r(pk, 0, 128), r(KB)], [r(OH)], lambda q, T, n=n, KB=KB, pk=pk, OH=OH: [q.tensor_tensor(T[OH][0:n, :], T[pk][0:n, 0:128], T[KB][0:n, :], O.is_equal)], "OH" + tag)
            oh = (b0, 384, 384 + n)
            PE(n, [r(OH), r("IB")], [r(*oh)], lambda q, T, n=n, OH=OH, oh=oh: [q.matmul(ap(oh)(T), T[OH][0:n, :], T.IB[0:n, 0:n], True, True)], 1, "OHA" + tag)
            if not last:
                either("OHA c%d" % c, v1(n), v1(n), [r(*oh)], [R("OHA")], copy(Q("OHA"), oh), act(Q("OHA"), oh, AF.Copy), "OHAe" + tag)
                tot = (b1, 128, 128 + n // 16)
                PE(64 * 17, [R("OHA"), r("isel"), r("IB"), r("VB")], [r(*tot)],
                   mm(tot, [("IB", ("VB", 0, n // 16))] + [(("isel", 128 * k, 128 * k + 128), ("OHA", a0 + k, a1, 16)) for k in range(16)]), 17, "to" + tag)
                V(tiny, [r(*tot)], [r("OT", h0, h1)], copy(("OT", h0, h1), tot), "OT" + tag)
                V(vg(n), [W("D"), W("D0"), r("OT", h0, h1), R("Z2")], [R("tt")], gtt(Q("tt"), ("D", c0, c1), ("OT", h0, h1), Q("Z2"), O.add), "tt" + tag)
                V(v1(n), [R("tt")], [R("Y2")], ts(Q("Y2"), Q("tt"), C24, O.add, -C24, O.add), "Y2" + tag)
            np_, nl_ = ("pk0", 256 + a0, 256 + a1), ("pb%d2" % b, 0, n)
            V(vg(n), [W("W"), r("OW", h0, h1), R("pas")], [R("R1")], gtt(Q("R1"), ("W", c0, c1), ("OW", h0, h1), Q("pas"), O.mult), "R1" + tag)
            V(v1(n), [r(*np_), R("cI")], [R("C1")], tt(Q("C1"), np_, Q("cI"), O.mult), "C1" + tag)
            V(v1(n), [r(*oh), R("cI")], [R("OC")], tt(Q("OC"), oh, Q("cI"), O.mult), "OC" + tag)
            PE(8 * n, [R("R1"), R("C1"), r("IF")], [r(*nl_)],
               lambda q, T, x=Q("R1"), y=Q("C1"), o=nl_: [q.matmul(ap(o)(T), T.IF[:], ap(x)(T), True, False), q.matmul(ap(o)(T), T.IF[:], ap(y)(T), False, False)], 2, "nl0" + tag)
            PE(4 * n, [R("OC"), r("Sel0"), r(*nl_)], [r(*nl_)], lambda q, T, x=Q("OC"), o=nl_: [q.matmul(ap(o)(T), T.Sel0[:], ap(x)(T), False, True)], 1, "nl1" + tag)
            if not last:
                V(v1(n), [r(*nl_)], [R(NU)], copy(Q(NU), nl_), "NU" + tag)
                add("g", 0.5, [R(NU)], [], ("send", t, c), "send" + tag, sem="sent")
            else:
                S(v1(n), [r(*nl_)], [R("yls")], act(Q("yls"), nl_, AF.Copy), "yls" + tag)
                dma("y", 2.0, [R("yls")], [], "ol%d" % c, lambda q, T, x=Q("yl"), y=Q("yls"): [q.dma_start(ap(x)(T), ap(y)(T))])
                S(v1(n), [W("ZS")], [R("yzs")], act(Q("yzs"), zs, AF.Copy), "yzs" + tag)
                dma("y", 2.0, [R("yzs")], [], "oz%d" % c, lambda q, T, x=Q("yz"), y=Q("yzs"): [q.dma_start(ap(x)(T), ap(y)(T))])
        if not last:
            tag = " t%d" % t
            sb = ("pb11", 144, 160)
            PE(64 * 16, [r("XL"), r("wsel")], [r(*sb)], mm(sb, [(("wsel", 128 * k, 128 * k + 128), ("XL", k, 256, 16)) for k in range(16)]), 16, "sb" + tag)
            V(tiny, [r(*sb)], [r("soA")], copy("soA", sb), "soA" + tag)
            V(tiny, [r("soA")], [r("soB")], ts("soB", "soA", 31, O.bitwise_and), "soB" + tag)
            V(tiny, [r("soB"), r("SOp")], [r("soC")], tt("soC", "soB", "SOp", O.add), "soC" + tag)
            V(tiny, [r("soC")], [r("SO")], copy("SO", "soC"), "SO" + tag)
            eb = ("pb11", 192, 256)
            PE(64 * 4, [r("pas"), r("S15")], [r(*eb)], mm(eb, [("S15", ("pas", 64 * k, 64 * k + 64)) for k in range(4)]), 4, "E" + tag)
            V(tiny, [r(*eb)], [r("er")], lambda q, T: [q.tensor_reduce(T.er[:], T.pb11[:, 192:256], AxisListType.X, O.add, negate=True)], "er" + tag)
            V(tiny, [r("er")], [r("eI")], copy("eI", "er"), "eI" + tag)
            V(tiny, [r("eI")], [r("eJ")], ts("eJ", "eI", 7, O.bitwise_and), "eJ" + tag)
            n1 = (t + 1, t + 2)
            who = [side("I c%d u%d" % (c, k)) for c, (a0, n, pcs) in enumerate(CHUNKS) for k in range(n // UNIT)]
            if "s" in who:
                V(tiny, [r("eJ"), r("nl")], [r("nth", *n1)], tt(("nth",) + n1, ("nl",) + n1, "eJ", O.subtract), "nth" + tag)
            if "v" in who:
                V(tiny, [r("eJ"), r("lf")], [r("thv", *n1)], tt(("thv",) + n1, ("lf",) + n1, "eJ", O.add), "thv" + tag)
            for c, (a0, n, pcs) in enumerate(CHUNKS):
                h0, h1 = a0 // 16, (a0 + n) // 16
                V(0.055 + 3.5 * n * cyc, [r("Y2", a0, a0 + n), r("half"), r("SO")], [r("X")],
                  lambda q, T, y=("Y2", a0, a0 + n), h=("half", 0, n), o=("SO", h0, h1): [q.tensor_tensor(T.X[:, 0:8192].indirect(ap(o)(T)), ap(y)(T), ap(h)(T), O.mult)], "scat c%d" % c + tag)
    return ops


def deps_of(ops):
    acc = {}
    for o in ops:
        d = set()
        for (b, lo, hi) in o["reads"]:
            for (p, l2, h2, w) in acc.get(b, []):
                if w and l2 < hi and lo < h2:
                    d.add((p, "raw"))
        for (b, lo, hi) in o["writes"]:
            for (p, l2, h2, w) in acc.get(b, []):
                if l2 < hi and lo < h2:
                    d.add((p, "waw" if w else "war"))
        for (b, lo, hi) in o["writes"]:
            acc[b] = [a for a in acc.get(b, []) if not (lo <= a[1] and a[2] <= hi)] + [(o["id"], lo, hi, True)]
        for (b, lo, hi) in o["reads"]:
            acc.setdefault(b, []).append((o["id"], lo, hi, False))
        o["deps"] = sorted((p, k) for (p, k) in d if p != o["id"])
        o["banks"] = sorted(set(b for (b, lo, hi) in o["reads"] + o["writes"] if b.startswith("pb") or b.startswith("pk")))
    return ops


def schedule(ops):
    n = len(ops)
    wake = P["wake"]
    succ = [[] for _ in range(n)]
    left = [0] * n
    for o in ops:
        ps = set(p for (p, k) in o["deps"])
        left[o["id"]] = len(ps)
        for p in ps:
            succ[p].append(o["id"])
    prio = [0.0] * n
    for o in reversed(ops):
        prio[o["id"]] = o["cost"] + max([prio[s] + wake for s in succ[o["id"]]], default=0.0) + PRI.get(o["name"].rsplit(" t", 1)[0], 0.0)
    fin = [0.0] * n
    start = [0.0] * n
    avail = [0.0] * n
    free = {"x": 0.0}
    bank = {}
    ready = [o["id"] for o in ops if left[o["id"]] == 0]
    order = []
    while ready:
        cand = []
        first = 1e9
        for i in ready:
            o = ops[i]
            e = o["eng"]
            st = max(avail[i], free.get(e, 0.0))
            for b in o["banks"]:
                for e2, f2 in bank.get(b, {}).items():
                    if e2 != e and f2 + wake > st:
                        st = f2 + wake
            cand.append((st, -prio[i], i))
            if st < first:
                first = st
        pr, st, i = min((p, s, j) for (s, p, j) in cand if s <= first + 0.03)
        o = ops[i]
        e = o["eng"]
        start[i] = st
        fin[i] = st + o["cost"]
        if o["sem"] and e in ("y", "s"):
            free[e] = st + 0.06 * o["n"]
        elif e != "x":
            free[e] = fin[i]
        for b in o["banks"]:
            bank.setdefault(b, {})[e] = fin[i]
        order.append(i)
        ready.remove(i)
        for s in succ[i]:
            left[s] -= 1
            if left[s] == 0:
                ready.append(s)
                a = 0.0
                for (p, k) in ops[s]["deps"]:
                    if not (k == "war" and ops[p]["eng"] == ops[s]["eng"]):
                        a = max(a, fin[p] + wake)
                avail[s] = a
    return order, start, fin


def free_steps():
    out = []
    for c, (a0, n, pcs) in enumerate(CHUNKS):
        for p in range(len(pcs)):
            out += ["%s c%d s%d" % (x, c, p) for x in ("G", "C", "A", "Z2")]
        out += ["I c%d u%d" % (c, k) for k in range(n // UNIT)] + ["%s c%d" % (x, c) for x in ("Z", "XL", "OHA")]
    return out


def step_names():
    keep, names = dict(PLACE), set()
    for e in "sv":
        for k in free_steps():
            PLACE[k] = e
        names |= set(o["name"].rsplit(" t", 1)[0] for o in build() if " t" in o["name"])
    PLACE.clear()
    PLACE.update(keep)
    return sorted(names)


PLACE.update(zip(free_steps(), SIDES))
PRI.update((k, int(x) / 10) for k, x in zip(step_names(), RANKS.split()))


def rank_program(g, core, T, topo):
    rank = T.rank_of(core)
    if rank is None:
        return
    cores = T.cores
    dst = cores[(rank + 1) % len(cores)]
    rid, pid, _ = topo.addr(dst)
    mask = topo.mask(core, dst)
    ne = len(topo.engines(core, dst))
    ni = len(topo.engines(cores[(rank - 1) % len(cores)], core))
    ops = deps_of(build())
    order = schedule(ops)[0]
    queues = {"v": g.vector, "s": g.scalar, "t": g.tensor, "g": g, "y": g.sync}
    csem = {"v": "cv", "s": "cs", "t": "ct", "g": "cg"}
    total = {}
    token = {}
    after = {}
    know = {e: {} for e in queues}
    lastbank = {}
    for i in order:
        o = ops[i]
        e = o["eng"]
        if e == "x":
            token[i] = (o["sem"], ni)
            total[o["sem"]] = ni
            after[i] = {}
            continue
        q = queues[e]
        need = {}
        ds = [p for (p, k) in o["deps"] if not (k == "war" and ops[p]["eng"] == e and token[p][0] == csem.get(e))]
        if e == "t":
            ds = [p for p in ds if ops[p]["eng"] != "t"]
        for b in o["banks"]:
            for e2, p in lastbank.get(b, {}).items():
                if e2 != e:
                    ds.append(p)
        inherit = []
        for p in ds:
            s, v = token[p]
            if know[e].get(s, 0) < v:
                need[s] = max(need.get(s, 0), v)
                inherit.append(p)
        for s in sorted(need):
            if any(after[p].get(s, 0) >= need[s] and token[p][0] != s for p in inherit):
                continue
            q.wait_ge(T.sem[s], int(need[s]))
        for p in inherit:
            s, v = token[p]
            for s2, v2 in list(after[p].items()) + [(s, v)]:
                if know[e].get(s2, 0) < v2:
                    know[e][s2] = v2
        after[i] = dict(know[e])
        if isinstance(o["fn"], tuple):
            _, t, c = o["fn"]
            a0, n, _ = CHUNKS[c]
            g.remote_dma(T["LU%d" % (t + 1)][:, a0:a0 + n], T["NU%d" % t][:, a0:a0 + n], T.sem["arr%d%d" % (t + 1, c)], T.sem["sent"], pid, rid, mask)
            total["sent"] = total.get("sent", 0) + ne
            token[i] = ("sent", total["sent"])
        else:
            ins = o["fn"](q, T)
            s, k = (o["sem"], 16) if o["sem"] else (csem[e], 1)
            for x in ins:
                x.then_inc(T.sem[s], k)
            total[s] = total.get(s, 0) + k * len(ins)
            token[i] = (s, total[s])
        for b in o["banks"]:
            lastbank.setdefault(b, {})[e] = i
    for s in sorted(total):
        g.wait_ge(T.sem[s], int(total[s]))
